import numpy as np
import ml_dtypes


def mxq(x, axis, fmt="e4m3"):
    dtype, down = {"e4m3": (ml_dtypes.float8_e4m3fn, 7), "e5m2": (ml_dtypes.float8_e5m2, 14)}[fmt]
    v = np.moveaxis(np.asarray(x, np.float32).astype(ml_dtypes.bfloat16).astype(np.float64), axis, -1)
    blocks = v.reshape(v.shape[:-1] + (-1, 32))
    amax = np.abs(blocks).max(-1, keepdims=True)
    byte = np.maximum(np.where(amax > 0, np.frexp(amax)[1] - 1 + 127, 0) - down, 1)
    scale = np.exp2(byte - 127.0)
    codes = (blocks / scale).astype(np.float32).astype(dtype).astype(np.float64)
    return np.moveaxis((codes * scale).reshape(v.shape), -1, axis)


WIDE = False


def mx_kscale(k):
    if not WIDE:
        return np.ones(k)
    levels = np.array([10, -10, 5, -5, 0])
    if k % 512:
        return np.exp2(np.random.permutation(np.resize(levels, k // 32))).repeat(32)
    a = np.empty((k // 512, 16))
    for p in range(k // 512):
        a[p, :8] = np.random.permutation(np.resize(levels, 8))
        for g in range(8):
            far = levels[np.abs(levels - a[p, g]) >= 10]
            a[p, g + 8] = far[np.random.randint(len(far))]
    return np.exp2(a.ravel()).repeat(32)


def f64(x):
    return np.asarray(x).astype(np.float64)


def striped(idx):
    return np.tile(idx.reshape(-1, 16).T, (8, 1)).astype(np.uint16)


def unstriped(offs):
    return offs[:16].T.reshape(-1).astype(np.int64)


E2M1 = np.array([0.0, 0.5, 1.0, 1.5, 2.0, 3.0, 4.0, 6.0, -0.0, -0.5, -1.0, -1.5, -2.0, -3.0, -4.0, -6.0])


def pack_weight(w, fmt):
    k, n = w.shape
    w = f64(np.asarray(w, np.float32).astype(ml_dtypes.bfloat16)).reshape(k // 32, 32, n)
    amax = np.abs(w).max(1)
    if fmt == "e4m3":
        byte = np.frexp(amax)[1] - 1 + 127 - 7
    else:
        mant, ex = np.frexp(amax / 6.0)
        byte = np.where(mant > 0.5, ex, ex - 1) + 127
    byte = np.clip(np.where(amax > 0, byte, 1), 1, 254)
    scaled = (w * np.exp2(127.0 - byte)[:, None, :]).reshape(k, n).astype(np.float32)
    by_word = np.ascontiguousarray(scaled.reshape(k // 512, 128, 4, n).transpose(0, 1, 3, 2))
    if fmt == "e4m3":
        words = by_word.astype(ml_dtypes.float8_e4m3fn).view(np.uint8)
    else:
        c = by_word.astype(ml_dtypes.float4_e2m1fn).view(np.uint8) & 0xF
        words = (c[..., 0::2] | (c[..., 1::2] << 4)).reshape(k // 512, 128, 2 * n)
    return np.ascontiguousarray(words), np.ascontiguousarray(byte.astype(np.uint8).reshape(k // 512, 16, n))


def unpack_weight(words, scales, fmt):
    g, _, n = scales.shape
    words = np.ascontiguousarray(words).reshape(g, 128, n, -1)
    if fmt == "e4m3":
        vals = words.view(ml_dtypes.float8_e4m3fn).astype(np.float64)
    else:
        nib = np.empty((g, 128, n, 4), np.uint8)
        nib[..., 0::2] = words & 0xF
        nib[..., 1::2] = words >> 4
        vals = E2M1[nib]
    vals = vals * np.repeat(np.exp2(scales.astype(np.float64) - 127.0), 8, axis=1)[..., None]
    return vals.transpose(0, 1, 3, 2).reshape(g * 512, n)


def gelu(v):
    return 0.5 * v * (1.0 + np.tanh(np.sqrt(2.0 / np.pi) * (v + 0.044715 * v**3)))


K, T, E, N = 1536, 1024, 4, 256
COUNTS = (384, 128, 256, 256)
STARTS = np.cumsum((0,) + COUNTS)
K8 = 512


def by_expert(wq, xq):
    return np.concatenate([wq[e].T @ xq[:, STARTS[e]:STARTS[e + 1]] for e in range(E)], axis=1)


def setup_inputs():
    n = np.random.standard_normal
    s = mx_kscale(K)[:, None]
    expert = np.random.permutation(np.repeat(np.arange(E), COUNTS))
    slot_token = np.argsort(expert, kind="stable")
    w = n((E, K, N)) / np.sqrt(K) / s[None]
    w8 = [pack_weight(m[:K8], "e4m3") for m in w]
    w4 = [pack_weight(m[K8:], "e2m1") for m in w]
    return {
        "xT": (n((K, T)) * s).astype(np.float32),
        "w8_words": np.stack([m[0] for m in w8]),
        "w8_scales": np.stack([m[1] for m in w8]),
        "w4_words": np.stack([m[0] for m in w4]),
        "w4_scales": np.stack([m[1] for m in w4]),
        "b": (0.3 * n((N, E))).astype(np.float32),
        "gate": np.tile(np.random.uniform(0.2, 1.0, T), (N, 1)).astype(np.float32),
        "offs": striped(slot_token),
    }


def reference(xT, w8_words, w8_scales, w4_words, w4_scales, b, gate, offs):
    idx = unstriped(offs)
    w = np.stack([np.concatenate([unpack_weight(w8_words[e], w8_scales[e], "e4m3"), unpack_weight(w4_words[e], w4_scales[e], "e2m1")]) for e in range(E)])
    xq = mxq(f64(xT)[:, idx], 0, "e4m3")
    y = by_expert(w, xq)
    y = gelu(y + np.repeat(f64(b), COUNTS, axis=1))
    out = np.zeros((N, T))
    out[:, idx] = f64(gate) * y
    return out

@@ -1,0 +1,171 @@
+from contextlib import ExitStack
+
+import concourse.mybir as mybir
+
+F32 = mybir.dt.float32
+BF16 = mybir.dt.bfloat16
+I32 = mybir.dt.int32
+U32 = mybir.dt.uint32
+U16 = mybir.dt.uint16
+U8 = mybir.dt.uint8
+FP8X4 = mybir.dt.float8_e4m3fn_x4
+FP4X4 = mybir.dt.float4_e2m1fn_x4
+ACT = mybir.ActivationFunctionType
+MULT = mybir.AluOpType.mult
+
+K, T, E, N = 1536, 1024, 4, 256
+COUNTS = (384, 128, 256, 256)
+STARTS = (0, 384, 512, 768)
+P = 128
+HALF = 512
+CHUNK = 128
+ORDER = (1, 2, 0)
+CHUNKS = (((0, 512, 192), (512, 256, 96), (768, 256, 96),), ((0, 512, 512), (512, 512, 448),), ((0, 512, 448), (512, 256, 192), (768, 256, 128),))
+
+FLOPS = 2 * K * N * T
+BYTES = 4 * K * T + E * (512 * N + 1024 * N // 2 + 48 * N) + 4 * N * E + 4 * T + 2 * P * 64 + 4 * N * T
+
+
+def expert_of(slot):
+    return max(e for e in range(E) if STARTS[e] <= slot)
+
+
+def tile_moe_rag_lin_gelu_kernel(
+    tc, xT, w8_words, w8_scales, w4_words, w4_scales, b, gate, offs, out
+):
+    nc = tc.nc
+    with ExitStack() as ctx:
+        keep = ctx.enter_context(tc.tile_pool(name="keep", bufs=1))
+        psum = ctx.enter_context(tc.psum_pool(name="psum", bufs=6))
+
+        offsets = keep.tile([P, T // 16], U16, name="offsets")
+
+        warm = keep.tile([P, 1], F32, name="warm")
+        warm_out = keep.tile([P, 1], F32, name="warm_out")
+        bytes_a = keep.tile([P, T], U8, name="bytes_a", align_bytes=64)
+        bytes_bc = keep.tile([P, T], U8, name="bytes_bc", align_bytes=64)
+        s8 = keep.tile([P, E, N], U8, name="s8", align_bytes=64)
+        s4 = keep.tile([P, 2 * E, N], U8, name="s4", align_bytes=64)
+        nc.gpsimd.memset(warm[:], 0.0)
+        nc.gpsimd.memset(bytes_a[:].bitcast(I32), 0)
+        nc.gpsimd.memset(bytes_bc[:].bitcast(I32), 0)
+        nc.gpsimd.memset(s4[:].rearrange("p e n -> p (e n)").bitcast(I32), 0)
+        nc.gpsimd.memset(s8[:].rearrange("p e n -> p (e n)").bitcast(I32), 0)
+        nc.scalar.activation(warm_out[:], warm[:], ACT.Gelu_apprx_tanh)
+
+        raws = {}
+        for i, a in enumerate(ORDER):
+            rows = xT[512 * a : 512 * (a + 1), :].rearrange("(p j) t -> p j t", j=4)
+            for lo, width, scalar in CHUNKS[i]:
+                raw = keep.tile([P, 4, width], F32, name=f"raw{i}_{lo}")
+                nc.sync.dma_start(raw[:], rows[:, :, lo : lo + width])
+                raws[i, lo] = raw
+            if i == 0:
+                nc.sync.dma_start(offsets[:], offs)
+        w4s = w4_scales.rearrange("e a q n -> (e a) q n")
+        for q in range(4):
+            src = w4s[:, 4 * q : 4 * q + 4, :].bitcast(I32)
+            nc.sync.dma_start(s4[32 * q : 32 * q + 4, :, :].bitcast(I32), src.rearrange("g r n -> r g n"))
+        for q in range(4):
+            src = w8_scales[:, 0, 4 * q : 4 * q + 4, :].bitcast(I32)
+            nc.sync.dma_start(s8[32 * q : 32 * q + 4, :, :].bitcast(I32), src.rearrange("e r n -> r e n"))
+        w8 = keep.tile([P, E, 4 * N], U8, name="w8", align_bytes=64)
+        w4 = keep.tile([P, E, 2, 2 * N], U8, name="w4", align_bytes=64)
+        gates = keep.tile([P, T], F32, name="gates")
+        bias = keep.tile([P, 2, E], F32, name="bias")
+        for h in range(2):
+            es = slice(2 * h, 2 * h + 2)
+            nc.sync.dma_start(
+                w4[:, es, :, :].rearrange("p e a x -> p (e a) x").bitcast(I32),
+                w4_words.rearrange("e a p x -> (e a) p x")[4 * h : 4 * h + 4].bitcast(I32).rearrange("g p x -> p g x"),
+            )
+            nc.sync.dma_start(
+                w8[:, es, :].bitcast(I32),
+                w8_words[es, 0].rearrange("e p n r -> e p (n r)").bitcast(I32).rearrange("e p x -> p e x"),
+            )
+            if h == 0:
+                nc.sync.dma_start(bias[:], b.rearrange("(m p) e -> p m e", p=P))
+            nc.sync.dma_start(gates[:, HALF * h : HALF * (h + 1)], gate[0:P, HALF * h : HALF * (h + 1)])
+
+        picked_a = keep.tile([P, T], U8, name="picked_a", align_bytes=64)
+        picked_bc = keep.tile([P, T], U8, name="picked_bc", align_bytes=64)
+        planes = (bytes_a[:], bytes_bc[:], bytes_bc[4:P, :])
+        picked_planes = (picked_a[:], picked_bc[:], picked_bc[4:P, :])
+        words = [keep.tile([P, T], U32, name=f"words{i}", align_bytes=64) for i in range(3)]
+        picked_words = [keep.tile([P, T], U32, name=f"picked_words{i}", align_bytes=64) for i in range(3)]
+
+        def group_and_quantize(i, lo, width, scalar):
+            grouped = keep.tile([P, width, 4], BF16, name=f"grouped{i}_{lo}", align_bytes=64)
+            raw = raws[i, lo]
+            for engine, u, v in ((nc.scalar, 0, scalar), (nc.vector, scalar, width)):
+                if u == v:
+                    continue
+                dst = grouped[:, u:v, :].rearrange("p (c i) j -> p c j i", i=4)
+                src = raw[:, :, u:v].rearrange("p j (c i) -> p c j i", i=4)
+                if engine is nc.scalar:
+                    nc.scalar.copy(dst, src)
+                else:
+                    nc.vector.tensor_copy(dst, src)
+            nc.vector.quantize_mx(
+                out=words[i][:, lo : lo + width].bitcast(FP8X4),
+                scales=planes[i][:, lo : lo + width],
+                in_=grouped[:].rearrange("p t j -> p (t j)"),
+            )
+
+        def pick(dst, src, h):
+            nc.vector.tensor_copy(dst[:, HALF * h : HALF * (h + 1)], src[:].indirect(offsets[:, 32 * h : 32 * (h + 1)]))
+
+        for i in range(3):
+            for n, chunk in enumerate(CHUNKS[i]):
+                group_and_quantize(i, *chunk)
+                if (i, n) == (2, 0):
+                    pick(picked_a, bytes_a, 0)
+                    pick(picked_a, bytes_a, 1)
+            for h in range(2):
+                pick(picked_words[i], words[i], h)
+                if i == 2:
+                    pick(picked_bc, bytes_bc, h)
+
+        def multiply(acc, m, slot, i):
+            e = expert_of(slot)
+            n_cols = slice(P * m, P * (m + 1))
+            s_cols = slice(slot, slot + CHUNK)
+            if i == 2:
+                lhs = w8[:, e, 4 * P * m : 4 * P * (m + 1)].bitcast(FP8X4)
+                lhs_scale = s8[:, e, n_cols]
+            else:
+                lhs = w4[:, e, i, 2 * P * m : 2 * P * (m + 1)].bitcast(FP4X4)
+                lhs_scale = s4[:, 2 * e + i, n_cols]
+            nc.tensor.matmul_mx(
+                out=acc,
+                lhsT=lhs,
+                lhsT_scale=lhs_scale,
+                rhs=picked_words[i][:, s_cols].bitcast(FP8X4),
+                rhs_scale=picked_planes[i][:, s_cols],
+                start=(i == 0),
+                stop=(i == 2),
+            )
+
+        y = [keep.tile([P, T], F32, name=f"y{m}") for m in range(2)]
+        result = [keep.tile([P, T], F32, name=f"result{m}") for m in range(2)]
+        for h in range(2):
+            slots = range(HALF * h, HALF * (h + 1), CHUNK)
+            for m in range(2):
+                accs = {}
+                for slot in slots:
+                    accs[slot] = psum.tile([P, CHUNK], F32, name="acc")
+                for i in range(3):
+                    for slot in slots:
+                        multiply(accs[slot][:], m, slot, i)
+                for slot in slots:
+                    e = expert_of(slot)
+                    nc.scalar.activation(
+                        y[m][:, slot : slot + CHUNK], accs[slot][:], ACT.Gelu_apprx_tanh, bias=bias[:, m, e : e + 1]
+                    )
+            for m in range(2):
+                cols = slice(HALF * h, HALF * (h + 1))
+                nc.vector.tensor_tensor(
+                    result[m][:].indirect(offsets[:, 32 * h : 32 * (h + 1)]), y[m][:, cols], gates[:, cols], MULT
+                )
+        for m in range(2):
+            nc.sync.dma_start(out[P * m : P * (m + 1), :], result[m][:])

@@ -17,10 +17,16 @@ K, T, E, N = 1536, 1024, 4, 256
 COUNTS = (384, 128, 256, 256)
 STARTS = (0, 384, 512, 768)
 P = 128
-HALF = 512
 CHUNK = 128
 ORDER = (1, 2, 0)
-CHUNKS = (((0, 512, 192), (512, 256, 96), (768, 256, 96),), ((0, 512, 512), (512, 512, 448),), ((0, 512, 448), (512, 256, 192), (768, 256, 128),))
+HALF = 512
+EARLY = 128
+EARLY_TOKENS = T - COUNTS[0] + EARLY
+LOADS = (
+    (((512, 192),), ((256, 96),), ((256, 128),)),
+    (((512, 512),), ((512, 320),)),
+    (((256, 256), (256, 256)), ((256, 128),), ((256, 256),)),
+)
 
 FLOPS = 2 * K * N * T
 BYTES = 4 * K * T + E * (512 * N + 1024 * N // 2 + 48 * N) + 4 * N * E + 4 * T + 2 * P * 64 + 4 * N * T
@@ -46,33 +52,34 @@ def tile_moe_rag_lin_gelu_kernel(
         bytes_bc = keep.tile([P, T], U8, name="bytes_bc", align_bytes=64)
         s8 = keep.tile([P, E, N], U8, name="s8", align_bytes=64)
         s4 = keep.tile([P, 2 * E, N], U8, name="s4", align_bytes=64)
+        words = [keep.tile([P, T], U32, name=f"words{i}", align_bytes=64) for i in range(3)]
         nc.gpsimd.memset(warm[:], 0.0)
-        nc.gpsimd.memset(bytes_a[:].bitcast(I32), 0)
-        nc.gpsimd.memset(bytes_bc[:].bitcast(I32), 0)
         nc.gpsimd.memset(s4[:].rearrange("p e n -> p (e n)").bitcast(I32), 0)
         nc.gpsimd.memset(s8[:].rearrange("p e n -> p (e n)").bitcast(I32), 0)
+        nc.gpsimd.memset(bytes_a[:].bitcast(I32), 0)
+        nc.gpsimd.memset(bytes_bc[:].bitcast(I32), 0)
         nc.scalar.activation(warm_out[:], warm[:], ACT.Gelu_apprx_tanh)
 
         raws = {}
+        bias = keep.tile([P, 2, E], F32, name="bias")
         for i, a in enumerate(ORDER):
             rows = xT[512 * a : 512 * (a + 1), :].rearrange("(p j) t -> p j t", j=4)
-            for lo, width, scalar in CHUNKS[i]:
+            lo = 0
+            for units in LOADS[i]:
+                width = sum(unit[0] for unit in units)
                 raw = keep.tile([P, 4, width], F32, name=f"raw{i}_{lo}")
                 nc.sync.dma_start(raw[:], rows[:, :, lo : lo + width])
                 raws[i, lo] = raw
-            if i == 0:
-                nc.sync.dma_start(offsets[:], offs)
+                if (i, lo) == (0, 512):
+                    nc.sync.dma_start(offsets[:], offs)
+                lo += width
         w4s = w4_scales.rearrange("e a q n -> (e a) q n")
         for q in range(4):
             src = w4s[:, 4 * q : 4 * q + 4, :].bitcast(I32)
             nc.sync.dma_start(s4[32 * q : 32 * q + 4, :, :].bitcast(I32), src.rearrange("g r n -> r g n"))
-        for q in range(4):
-            src = w8_scales[:, 0, 4 * q : 4 * q + 4, :].bitcast(I32)
-            nc.sync.dma_start(s8[32 * q : 32 * q + 4, :, :].bitcast(I32), src.rearrange("e r n -> r e n"))
         w8 = keep.tile([P, E, 4 * N], U8, name="w8", align_bytes=64)
         w4 = keep.tile([P, E, 2, 2 * N], U8, name="w4", align_bytes=64)
         gates = keep.tile([P, T], F32, name="gates")
-        bias = keep.tile([P, 2, E], F32, name="bias")
         for h in range(2):
             es = slice(2 * h, 2 * h + 2)
             nc.sync.dma_start(
@@ -83,25 +90,26 @@ def tile_moe_rag_lin_gelu_kernel(
                 w8[:, es, :].bitcast(I32),
                 w8_words[es, 0].rearrange("e p n r -> e p (n r)").bitcast(I32).rearrange("e p x -> p e x"),
             )
-            if h == 0:
-                nc.sync.dma_start(bias[:], b.rearrange("(m p) e -> p m e", p=P))
             nc.sync.dma_start(gates[:, HALF * h : HALF * (h + 1)], gate[0:P, HALF * h : HALF * (h + 1)])
+            if h == 0:
+                for q in range(4):
+                    src = w8_scales[:, 0, 4 * q : 4 * q + 4, :].bitcast(I32)
+                    nc.sync.dma_start(s8[32 * q : 32 * q + 4, :, :].bitcast(I32), src.rearrange("e r n -> r e n"))
+                nc.sync.dma_start(bias[:], b.rearrange("(m p) e -> p m e", p=P))
 
         picked_a = keep.tile([P, T], U8, name="picked_a", align_bytes=64)
         picked_bc = keep.tile([P, T], U8, name="picked_bc", align_bytes=64)
         planes = (bytes_a[:], bytes_bc[:], bytes_bc[4:P, :])
         picked_planes = (picked_a[:], picked_bc[:], picked_bc[4:P, :])
-        words = [keep.tile([P, T], U32, name=f"words{i}", align_bytes=64) for i in range(3)]
         picked_words = [keep.tile([P, T], U32, name=f"picked_words{i}", align_bytes=64) for i in range(3)]
 
-        def group_and_quantize(i, lo, width, scalar):
+        def group_and_quantize(i, raw, at, lo, width, scalar):
             grouped = keep.tile([P, width, 4], BF16, name=f"grouped{i}_{lo}", align_bytes=64)
-            raw = raws[i, lo]
             for engine, u, v in ((nc.scalar, 0, scalar), (nc.vector, scalar, width)):
                 if u == v:
                     continue
                 dst = grouped[:, u:v, :].rearrange("p (c i) j -> p c j i", i=4)
-                src = raw[:, :, u:v].rearrange("p j (c i) -> p c j i", i=4)
+                src = raw[:, :, at + u : at + v].rearrange("p j (c i) -> p c j i", i=4)
                 if engine is nc.scalar:
                     nc.scalar.copy(dst, src)
                 else:
@@ -112,19 +120,26 @@ def tile_moe_rag_lin_gelu_kernel(
                 in_=grouped[:].rearrange("p t j -> p (t j)"),
             )
 
-        def pick(dst, src, h):
-            nc.vector.tensor_copy(dst[:, HALF * h : HALF * (h + 1)], src[:].indirect(offsets[:, 32 * h : 32 * (h + 1)]))
+        def pick(dst, window, lo, hi):
+            nc.vector.tensor_copy(dst[:, lo:hi], window.indirect(offsets[:, lo // 16 : hi // 16]))
 
+        packed = (bytes_a, None, bytes_bc)
+        picked_packed = (picked_a, None, picked_bc)
         for i in range(3):
-            for n, chunk in enumerate(CHUNKS[i]):
-                group_and_quantize(i, *chunk)
-                if (i, n) == (2, 0):
-                    pick(picked_a, bytes_a, 0)
-                    pick(picked_a, bytes_a, 1)
-            for h in range(2):
-                pick(picked_words[i], words[i], h)
-                if i == 2:
-                    pick(picked_bc, bytes_bc, h)
+            lo = 0
+            for units in LOADS[i]:
+                raw, at = raws[i, lo], 0
+                for width, scalar in units:
+                    group_and_quantize(i, raw, at, lo, width, scalar)
+                    at += width
+                    lo += width
+                if i != 1 and lo == EARLY_TOKENS:
+                    pick(picked_packed[i], packed[i][:, 0:lo], 0, EARLY)
+                    pick(picked_words[i], words[i][:, 0:lo], 0, EARLY)
+            for u, v in ((0 if i == 1 else EARLY, HALF), (HALF, T)):
+                if i != 1:
+                    pick(picked_packed[i], packed[i][:], u, v)
+                pick(picked_words[i], words[i][:], u, v)
 
         def multiply(acc, m, slot, i):
             e = expert_of(slot)
@@ -148,8 +163,8 @@ def tile_moe_rag_lin_gelu_kernel(
 
         y = [keep.tile([P, T], F32, name=f"y{m}") for m in range(2)]
         result = [keep.tile([P, T], F32, name=f"result{m}") for m in range(2)]
-        for h in range(2):
-            slots = range(HALF * h, HALF * (h + 1), CHUNK)
+        for lo, hi in ((0, HALF), (HALF, T)):
+            slots = range(lo, hi, CHUNK)
             for m in range(2):
                 accs = {}
                 for slot in slots:
@@ -163,9 +178,8 @@ def tile_moe_rag_lin_gelu_kernel(
                         y[m][:, slot : slot + CHUNK], accs[slot][:], ACT.Gelu_apprx_tanh, bias=bias[:, m, e : e + 1]
                     )
             for m in range(2):
-                cols = slice(HALF * h, HALF * (h + 1))
                 nc.vector.tensor_tensor(
-                    result[m][:].indirect(offsets[:, 32 * h : 32 * (h + 1)]), y[m][:, cols], gates[:, cols], MULT
+                    result[m][:].indirect(offsets[:, lo // 16 : hi // 16]), y[m][:, lo:hi], gates[:, lo:hi], MULT
                 )
         for m in range(2):
             nc.sync.dma_start(out[P * m : P * (m + 1), :], result[m][:])

@@ -20,12 +20,13 @@ P = 128
 CHUNK = 128
 ORDER = (1, 2, 0)
 HALF = 512
+WIDE = 1408
 EARLY = 128
 EARLY_TOKENS = T - COUNTS[0] + EARLY
 LOADS = (
-    (((512, 192),), ((256, 96),), ((256, 128),)),
-    (((512, 512),), ((512, 320),)),
-    (((256, 256), (256, 256)), ((256, 128),), ((256, 256),)),
+    (((256, 0), (256, 256)), ((256, 128),), ((256, 160),)),
+    (((512, 512),), ((512, 352),)),
+    (((512, 512),), ((256, 192),), ((256, 256),)),
 )
 
 FLOPS = 2 * K * N * T
@@ -48,16 +49,18 @@ def tile_moe_rag_lin_gelu_kernel(
 
         warm = keep.tile([P, 1], F32, name="warm")
         warm_out = keep.tile([P, 1], F32, name="warm_out")
-        bytes_a = keep.tile([P, T], U8, name="bytes_a", align_bytes=64)
+        bytes_a = keep.tile([P, WIDE], U8, name="bytes_a", align_bytes=64)
         bytes_bc = keep.tile([P, T], U8, name="bytes_bc", align_bytes=64)
         s8 = keep.tile([P, E, N], U8, name="s8", align_bytes=64)
         s4 = keep.tile([P, 2 * E, N], U8, name="s4", align_bytes=64)
-        words = [keep.tile([P, T], U32, name=f"words{i}", align_bytes=64) for i in range(3)]
+        words = [keep.tile([P, WIDE if i < 2 else T], U32, name=f"words{i}", align_bytes=64) for i in range(3)]
         nc.gpsimd.memset(warm[:], 0.0)
         nc.gpsimd.memset(s4[:].rearrange("p e n -> p (e n)").bitcast(I32), 0)
         nc.gpsimd.memset(s8[:].rearrange("p e n -> p (e n)").bitcast(I32), 0)
         nc.gpsimd.memset(bytes_a[:].bitcast(I32), 0)
+        nc.gpsimd.memset(words[0][:, T:WIDE].bitcast(I32), 0)
         nc.gpsimd.memset(bytes_bc[:].bitcast(I32), 0)
+        nc.gpsimd.memset(words[1][:, T:WIDE].bitcast(I32), 0)
         nc.scalar.activation(warm_out[:], warm[:], ACT.Gelu_apprx_tanh)
 
         raws = {}
@@ -136,7 +139,7 @@ def tile_moe_rag_lin_gelu_kernel(
                 if i != 1 and lo == EARLY_TOKENS:
                     pick(picked_packed[i], packed[i][:, 0:lo], 0, EARLY)
                     pick(picked_words[i], words[i][:, 0:lo], 0, EARLY)
-            for u, v in ((0 if i == 1 else EARLY, HALF), (HALF, T)):
+            for u, v in (((EARLY, T),), ((0, T),), ((EARLY, HALF), (HALF, T)))[i]:
                 if i != 1:
                     pick(picked_packed[i], packed[i][:], u, v)
                 pick(picked_words[i], words[i][:], u, v)

@@ -24,9 +24,9 @@ WIDE = 1408
 EARLY = 128
 EARLY_TOKENS = T - COUNTS[0] + EARLY
 LOADS = (
-    (((256, 0), (256, 256)), ((256, 128),), ((256, 160),)),
-    (((512, 512),), ((512, 352),)),
-    (((512, 512),), ((256, 192),), ((256, 256),)),
+    (((256, 0), (256, 256), (256, 0), (256, 256)),),
+    (((512, 512),), ((512, 512),)),
+    (((512, 512),), ((256, 256),), ((256, 256),)),
 )
 
 FLOPS = 2 * K * N * T
@@ -47,21 +47,17 @@ def tile_moe_rag_lin_gelu_kernel(
 
         offsets = keep.tile([P, T // 16], U16, name="offsets")
 
-        warm = keep.tile([P, 1], F32, name="warm")
-        warm_out = keep.tile([P, 1], F32, name="warm_out")
         bytes_a = keep.tile([P, WIDE], U8, name="bytes_a", align_bytes=64)
         bytes_bc = keep.tile([P, T], U8, name="bytes_bc", align_bytes=64)
         s8 = keep.tile([P, E, N], U8, name="s8", align_bytes=64)
         s4 = keep.tile([P, 2 * E, N], U8, name="s4", align_bytes=64)
         words = [keep.tile([P, WIDE if i < 2 else T], U32, name=f"words{i}", align_bytes=64) for i in range(3)]
-        nc.gpsimd.memset(warm[:], 0.0)
         nc.gpsimd.memset(s4[:].rearrange("p e n -> p (e n)").bitcast(I32), 0)
         nc.gpsimd.memset(s8[:].rearrange("p e n -> p (e n)").bitcast(I32), 0)
         nc.gpsimd.memset(bytes_a[:].bitcast(I32), 0)
         nc.gpsimd.memset(words[0][:, T:WIDE].bitcast(I32), 0)
         nc.gpsimd.memset(bytes_bc[:].bitcast(I32), 0)
         nc.gpsimd.memset(words[1][:, T:WIDE].bitcast(I32), 0)
-        nc.scalar.activation(warm_out[:], warm[:], ACT.Gelu_apprx_tanh)
 
         raws = {}
         bias = keep.tile([P, 2, E], F32, name="bias")
@@ -73,7 +69,7 @@ def tile_moe_rag_lin_gelu_kernel(
                 raw = keep.tile([P, 4, width], F32, name=f"raw{i}_{lo}")
                 nc.sync.dma_start(raw[:], rows[:, :, lo : lo + width])
                 raws[i, lo] = raw
-                if (i, lo) == (0, 512):
+                if i == 0:
                     nc.sync.dma_start(offsets[:], offs)
                 lo += width
         w4s = w4_scales.rearrange("e a q n -> (e a) q n")
@@ -136,10 +132,10 @@ def tile_moe_rag_lin_gelu_kernel(
                     group_and_quantize(i, raw, at, lo, width, scalar)
                     at += width
                     lo += width
-                if i != 1 and lo == EARLY_TOKENS:
+                if i == 2 and lo == EARLY_TOKENS:
                     pick(picked_packed[i], packed[i][:, 0:lo], 0, EARLY)
                     pick(picked_words[i], words[i][:, 0:lo], 0, EARLY)
-            for u, v in (((EARLY, T),), ((0, T),), ((EARLY, HALF), (HALF, T)))[i]:
+            for u, v in (((0, T),), ((0, T),), ((EARLY, HALF), (HALF, T)))[i]:
                 if i != 1:
                     pick(picked_packed[i], packed[i][:], u, v)
                 pick(picked_words[i], words[i][:], u, v)

@@ -19,14 +19,17 @@ STARTS = (0, 384, 512, 768)
 P = 128
 CHUNK = 128
 ORDER = (1, 2, 0)
-HALF = 512
 WIDE = 1408
+RESULT_WIDE = 1280
+FIRST = COUNTS[0]
+PIECES = ((0, FIRST), (FIRST, T))
+PIECE_EXPERTS = ((0, 1), (1, E))
 EARLY = 128
 EARLY_TOKENS = T - COUNTS[0] + EARLY
 LOADS = (
     (((256, 0), (256, 256), (256, 0), (256, 256)),),
     (((512, 512),), ((512, 512),)),
-    (((512, 512),), ((256, 256),), ((256, 256),)),
+    (((512, 384),), ((256, 256),), ((256, 192),)),
 )
 
 FLOPS = 2 * K * N * T
@@ -79,22 +82,23 @@ def tile_moe_rag_lin_gelu_kernel(
         w8 = keep.tile([P, E, 4 * N], U8, name="w8", align_bytes=64)
         w4 = keep.tile([P, E, 2, 2 * N], U8, name="w4", align_bytes=64)
         gates = keep.tile([P, T], F32, name="gates")
-        for h in range(2):
-            es = slice(2 * h, 2 * h + 2)
+        for h, (e0, e1) in enumerate(PIECE_EXPERTS):
+            es = slice(e0, e1)
+            g_cols = slice(*PIECES[h])
             nc.sync.dma_start(
                 w4[:, es, :, :].rearrange("p e a x -> p (e a) x").bitcast(I32),
-                w4_words.rearrange("e a p x -> (e a) p x")[4 * h : 4 * h + 4].bitcast(I32).rearrange("g p x -> p g x"),
+                w4_words.rearrange("e a p x -> (e a) p x")[2 * e0 : 2 * e1].bitcast(I32).rearrange("g p x -> p g x"),
             )
             nc.sync.dma_start(
                 w8[:, es, :].bitcast(I32),
                 w8_words[es, 0].rearrange("e p n r -> e p (n r)").bitcast(I32).rearrange("e p x -> p e x"),
             )
-            nc.sync.dma_start(gates[:, HALF * h : HALF * (h + 1)], gate[0:P, HALF * h : HALF * (h + 1)])
             if h == 0:
                 for q in range(4):
                     src = w8_scales[:, 0, 4 * q : 4 * q + 4, :].bitcast(I32)
                     nc.sync.dma_start(s8[32 * q : 32 * q + 4, :, :].bitcast(I32), src.rearrange("e r n -> r e n"))
                 nc.sync.dma_start(bias[:], b.rearrange("(m p) e -> p m e", p=P))
+            nc.sync.dma_start(gates[:, g_cols], gate[0:P, g_cols])
 
         picked_a = keep.tile([P, T], U8, name="picked_a", align_bytes=64)
         picked_bc = keep.tile([P, T], U8, name="picked_bc", align_bytes=64)
@@ -135,7 +139,7 @@ def tile_moe_rag_lin_gelu_kernel(
                 if i == 2 and lo == EARLY_TOKENS:
                     pick(picked_packed[i], packed[i][:, 0:lo], 0, EARLY)
                     pick(picked_words[i], words[i][:, 0:lo], 0, EARLY)
-            for u, v in (((0, T),), ((0, T),), ((EARLY, HALF), (HALF, T)))[i]:
+            for u, v in (((0, T),), ((0, T),), ((EARLY, FIRST), (FIRST, T)))[i]:
                 if i != 1:
                     pick(picked_packed[i], packed[i][:], u, v)
                 pick(picked_words[i], words[i][:], u, v)
@@ -161,8 +165,8 @@ def tile_moe_rag_lin_gelu_kernel(
             )
 
         y = [keep.tile([P, T], F32, name=f"y{m}") for m in range(2)]
-        result = [keep.tile([P, T], F32, name=f"result{m}") for m in range(2)]
-        for lo, hi in ((0, HALF), (HALF, T)):
+        result = [keep.tile([P, RESULT_WIDE], F32, name=f"result{m}") for m in range(2)]
+        for lo, hi in PIECES:
             slots = range(lo, hi, CHUNK)
             for m in range(2):
                 accs = {}
@@ -181,4 +185,4 @@ def tile_moe_rag_lin_gelu_kernel(
                     result[m][:].indirect(offsets[:, lo // 16 : hi // 16]), y[m][:, lo:hi], gates[:, lo:hi], MULT
                 )
         for m in range(2):
-            nc.sync.dma_start(out[P * m : P * (m + 1), :], result[m][:])
+            nc.sync.dma_start(out[P * m : P * (m + 1), :], result[m][:, 0:T])

@@ -27,9 +27,9 @@ PIECE_EXPERTS = ((0, 1), (1, E))
 EARLY = 128
 EARLY_TOKENS = T - COUNTS[0] + EARLY
 LOADS = (
-    (((256, 0), (256, 256), (256, 0), (256, 256)),),
-    (((512, 512),), ((512, 512),)),
-    (((512, 384),), ((256, 256),), ((256, 192),)),
+    (((512, 0), (256, 256), (256, 192)),),
+    (((512, 512),), ((256, 256), (256, 192))),
+    (((256, 256), (256, 96)), ((256, 256),), ((128, 128), (128, 128))),
 )
 
 FLOPS = 2 * K * N * T
@@ -106,7 +106,7 @@ def tile_moe_rag_lin_gelu_kernel(
         picked_planes = (picked_a[:], picked_bc[:], picked_bc[4:P, :])
         picked_words = [keep.tile([P, T], U32, name=f"picked_words{i}", align_bytes=64) for i in range(3)]
 
-        def group_and_quantize(i, raw, at, lo, width, scalar):
+        def group(i, raw, at, lo, width, scalar):
             grouped = keep.tile([P, width, 4], BF16, name=f"grouped{i}_{lo}", align_bytes=64)
             for engine, u, v in ((nc.scalar, 0, scalar), (nc.vector, scalar, width)):
                 if u == v:
@@ -117,6 +117,9 @@ def tile_moe_rag_lin_gelu_kernel(
                     nc.scalar.copy(dst, src)
                 else:
                     nc.vector.tensor_copy(dst, src)
+            return grouped
+
+        def quantize(i, grouped, lo, width):
             nc.vector.quantize_mx(
                 out=words[i][:, lo : lo + width].bitcast(FP8X4),
                 scales=planes[i][:, lo : lo + width],
@@ -131,11 +134,13 @@ def tile_moe_rag_lin_gelu_kernel(
         for i in range(3):
             lo = 0
             for units in LOADS[i]:
-                raw, at = raws[i, lo], 0
+                raw, at, ready = raws[i, lo], 0, []
                 for width, scalar in units:
-                    group_and_quantize(i, raw, at, lo, width, scalar)
+                    ready.append((group(i, raw, at, lo, width, scalar), lo, width))
                     at += width
                     lo += width
+                for grouped, start, width in ready:
+                    quantize(i, grouped, start, width)
                 if i == 2 and lo == EARLY_TOKENS:
                     pick(picked_packed[i], packed[i][:, 0:lo], 0, EARLY)
                     pick(picked_words[i], words[i][:, 0:lo], 0, EARLY)

@@ -28,8 +28,8 @@ EARLY = 128
 EARLY_TOKENS = T - COUNTS[0] + EARLY
 LOADS = (
     (((512, 0), (256, 256), (256, 192)),),
-    (((512, 512),), ((256, 256), (256, 192))),
-    (((256, 256), (256, 96)), ((256, 256),), ((128, 128), (128, 128))),
+    (((512, 512),), ((256, 256), (256, 256))),
+    (((256, 256), (256, 128)), ((256, 256),), ((128, 128), (128, 128))),
 )
 
 FLOPS = 2 * K * N * T

@@ -29,7 +29,7 @@ EARLY_TOKENS = T - COUNTS[0] + EARLY
 LOADS = (
     (((512, 0), (256, 256), (256, 192)),),
     (((512, 512),), ((256, 256), (256, 256))),
-    (((256, 256), (256, 128)), ((256, 256),), ((128, 128), (128, 128))),
+    (((256, 256), (256, -1)), ((256, 256),), ((128, 128), (128, 128))),
 )
 
 FLOPS = 2 * K * N * T
@@ -107,7 +107,13 @@ def tile_moe_rag_lin_gelu_kernel(
         picked_words = [keep.tile([P, T], U32, name=f"picked_words{i}", align_bytes=64) for i in range(3)]
 
         def group(i, raw, at, lo, width, scalar):
-            grouped = keep.tile([P, width, 4], BF16, name=f"grouped{i}_{lo}", align_bytes=64)
+            shared = scalar < 0 or (i, lo) == (1, 768)
+            grouped = keep.tile([P, width, 4], BF16, name="grouped_shared" if shared else f"grouped{i}_{lo}", align_bytes=64)
+            if scalar < 0:
+                nc.gpsimd.tensor_copy(
+                    grouped[:], raw[:, :, at : at + width].rearrange("p j t -> p t j")
+                )
+                return grouped
             for engine, u, v in ((nc.scalar, 0, scalar), (nc.vector, scalar, width)):
                 if u == v:
                     continue

@@ -27,10 +27,11 @@ PIECE_EXPERTS = ((0, 1), (1, E))
 EARLY = 128
 EARLY_TOKENS = T - COUNTS[0] + EARLY
 LOADS = (
-    (((512, 0), (256, 256), (256, 192)),),
-    (((512, 512),), ((256, 256), (256, 256))),
-    (((256, 256), (256, -1)), ((256, 256),), ((128, 128), (128, 128))),
+    ((((512, 448, 0), (256, 0, 0), (256, 96, 0)),),),
+    ((((256, 0, 0), (256, 0, 256)),), (((256, 0, 0), (256, 0, 96)),)),
+    ((((256, 0, 0), (256, 0, 192)),), (((256, 0, 0),),), (((128, 0, 0), (128, 0, 64)),)),
 )
+TAKES_OVER = {(1, 256): (0, 768), (2, 256): (1, 768), (2, 896): (2, 512)}
 
 FLOPS = 2 * K * N * T
 BYTES = 4 * K * T + E * (512 * N + 1024 * N // 2 + 48 * N) + 4 * N * E + 4 * T + 2 * P * 64 + 4 * N * T
@@ -67,10 +68,21 @@ def tile_moe_rag_lin_gelu_kernel(
         for i, a in enumerate(ORDER):
             rows = xT[512 * a : 512 * (a + 1), :].rearrange("(p j) t -> p j t", j=4)
             lo = 0
-            for units in LOADS[i]:
-                width = sum(unit[0] for unit in units)
+            for steps in LOADS[i]:
+                widths = [sum(unit[0] for unit in units) for units in steps]
+                width = sum(widths)
                 raw = keep.tile([P, 4, width], F32, name=f"raw{i}_{lo}")
-                nc.sync.dma_start(raw[:], rows[:, :, lo : lo + width])
+                if len(steps) == 1:
+                    nc.sync.dma_start(raw[:], rows[:, :, lo : lo + width])
+                else:
+                    flat_src = rows.rearrange("p j t -> p (j t)")
+                    flat_dst = raw[:].rearrange("p j t -> p (j t)")
+                    u = 0
+                    v = 3 * T
+                    for step in widths:
+                        v += step
+                        nc.sync.dma_start(flat_dst[:, u:v], flat_src[:, u:v])
+                        u = v
                 raws[i, lo] = raw
                 if i == 0:
                     nc.sync.dma_start(offsets[:], offs)
@@ -106,15 +118,14 @@ def tile_moe_rag_lin_gelu_kernel(
         picked_planes = (picked_a[:], picked_bc[:], picked_bc[4:P, :])
         picked_words = [keep.tile([P, T], U32, name=f"picked_words{i}", align_bytes=64) for i in range(3)]
 
-        def group(i, raw, at, lo, width, scalar):
-            shared = scalar < 0 or (i, lo) == (1, 768)
-            grouped = keep.tile([P, width, 4], BF16, name="grouped_shared" if shared else f"grouped{i}_{lo}", align_bytes=64)
-            if scalar < 0:
-                nc.gpsimd.tensor_copy(
-                    grouped[:], raw[:, :, at : at + width].rearrange("p j t -> p t j")
-                )
-                return grouped
-            for engine, u, v in ((nc.scalar, 0, scalar), (nc.vector, scalar, width)):
+        def group(i, raw, at, lo, width, vector, gpsimd):
+            owner = TAKES_OVER.get((i, lo), (i, lo))
+            grouped = keep.tile([P, width, 4], BF16, name=f"grouped{owner[0]}_{owner[1]}", align_bytes=64)
+            scalar = width - vector - gpsimd
+            if gpsimd:
+                u, v = scalar, scalar + gpsimd
+                nc.gpsimd.tensor_copy(grouped[:, u:v, :], raw[:, :, at + u : at + v].rearrange("p j t -> p t j"))
+            for engine, u, v in ((nc.scalar, 0, scalar), (nc.vector, scalar + gpsimd, width)):
                 if u == v:
                     continue
                 dst = grouped[:, u:v, :].rearrange("p (c i) j -> p c j i", i=4)
@@ -139,14 +150,16 @@ def tile_moe_rag_lin_gelu_kernel(
         picked_packed = (picked_a, None, picked_bc)
         for i in range(3):
             lo = 0
-            for units in LOADS[i]:
-                raw, at, ready = raws[i, lo], 0, []
-                for width, scalar in units:
-                    ready.append((group(i, raw, at, lo, width, scalar), lo, width))
-                    at += width
-                    lo += width
-                for grouped, start, width in ready:
-                    quantize(i, grouped, start, width)
+            for steps in LOADS[i]:
+                raw, at = raws[i, lo], 0
+                for units in steps:
+                    ready = []
+                    for width, vector, gpsimd in units:
+                        ready.append((group(i, raw, at, lo, width, vector, gpsimd), lo, width))
+                        at += width
+                        lo += width
+                    for grouped, start, width in ready:
+                        quantize(i, grouped, start, width)
                 if i == 2 and lo == EARLY_TOKENS:
                     pick(picked_packed[i], packed[i][:, 0:lo], 0, EARLY)
                     pick(picked_words[i], words[i][:, 0:lo], 0, EARLY)

@@ -24,6 +24,8 @@ RESULT_WIDE = 1280
 FIRST = COUNTS[0]
 PIECES = ((0, FIRST), (FIRST, T))
 PIECE_EXPERTS = ((0, 1), (1, E))
+BANKS = (((0, 384),), ((384, 768), (768, 1024)))
+PASS_ORDER = ((0, 1, 2), (1, 0, 2))
 EARLY = 128
 EARLY_TOKENS = T - COUNTS[0] + EARLY
 LOADS = (
@@ -47,7 +49,7 @@ def tile_moe_rag_lin_gelu_kernel(
     nc = tc.nc
     with ExitStack() as ctx:
         keep = ctx.enter_context(tc.tile_pool(name="keep", bufs=1))
-        psum = ctx.enter_context(tc.psum_pool(name="psum", bufs=6))
+        psum = ctx.enter_context(tc.psum_pool(name="psum", bufs=1))
 
         offsets = keep.tile([P, T // 16], U16, name="offsets")
 
@@ -56,12 +58,19 @@ def tile_moe_rag_lin_gelu_kernel(
         s8 = keep.tile([P, E, N], U8, name="s8", align_bytes=64)
         s4 = keep.tile([P, 2 * E, N], U8, name="s4", align_bytes=64)
         words = [keep.tile([P, WIDE if i < 2 else T], U32, name=f"words{i}", align_bytes=64) for i in range(3)]
-        nc.gpsimd.memset(s4[:].rearrange("p e n -> p (e n)").bitcast(I32), 0)
         nc.gpsimd.memset(s8[:].rearrange("p e n -> p (e n)").bitcast(I32), 0)
+        nc.gpsimd.memset(s4[:].rearrange("p e n -> p (e n)").bitcast(I32), 0)
         nc.gpsimd.memset(bytes_a[:].bitcast(I32), 0)
         nc.gpsimd.memset(words[0][:, T:WIDE].bitcast(I32), 0)
         nc.gpsimd.memset(bytes_bc[:].bitcast(I32), 0)
         nc.gpsimd.memset(words[1][:, T:WIDE].bitcast(I32), 0)
+
+        for q in range(4):
+            src = w8_scales[:, 0, 4 * q : 4 * q + 4, :].bitcast(I32)
+            nc.scalar.dma_start(s8[32 * q : 32 * q + 4, :, :].bitcast(I32), src.rearrange("e r n -> r e n"))
+        warm = keep.tile([P, 2], F32, name="warm")
+        nc.vector.memset(warm[:, 0:1], 0.0)
+        nc.scalar.activation(warm[:, 1:2], warm[:, 0:1], ACT.Gelu_apprx_tanh)
 
         raws = {}
         bias = keep.tile([P, 2, E], F32, name="bias")
@@ -106,9 +115,6 @@ def tile_moe_rag_lin_gelu_kernel(
                 w8_words[es, 0].rearrange("e p n r -> e p (n r)").bitcast(I32).rearrange("e p x -> p e x"),
             )
             if h == 0:
-                for q in range(4):
-                    src = w8_scales[:, 0, 4 * q : 4 * q + 4, :].bitcast(I32)
-                    nc.sync.dma_start(s8[32 * q : 32 * q + 4, :, :].bitcast(I32), src.rearrange("e r n -> r e n"))
                 nc.sync.dma_start(bias[:], b.rearrange("(m p) e -> p m e", p=P))
             nc.sync.dma_start(gates[:, g_cols], gate[0:P, g_cols])
 
@@ -168,7 +174,7 @@ def tile_moe_rag_lin_gelu_kernel(
                     pick(picked_packed[i], packed[i][:], u, v)
                 pick(picked_words[i], words[i][:], u, v)
 
-        def multiply(acc, m, slot, i):
+        def multiply(acc, m, slot, i, start, stop):
             e = expert_of(slot)
             n_cols = slice(P * m, P * (m + 1))
             s_cols = slice(slot, slot + CHUNK)
@@ -184,26 +190,28 @@ def tile_moe_rag_lin_gelu_kernel(
                 lhsT_scale=lhs_scale,
                 rhs=picked_words[i][:, s_cols].bitcast(FP8X4),
                 rhs_scale=picked_planes[i][:, s_cols],
-                start=(i == 0),
-                stop=(i == 2),
+                start=start,
+                stop=stop,
             )
 
         y = [keep.tile([P, T], F32, name=f"y{m}") for m in range(2)]
         result = [keep.tile([P, RESULT_WIDE], F32, name=f"result{m}") for m in range(2)]
-        for lo, hi in PIECES:
-            slots = range(lo, hi, CHUNK)
+        for (lo, hi), banks, order in zip(PIECES, BANKS, PASS_ORDER):
             for m in range(2):
-                accs = {}
-                for slot in slots:
-                    accs[slot] = psum.tile([P, CHUNK], F32, name="acc")
-                for i in range(3):
-                    for slot in slots:
-                        multiply(accs[slot][:], m, slot, i)
-                for slot in slots:
-                    e = expert_of(slot)
-                    nc.scalar.activation(
-                        y[m][:, slot : slot + CHUNK], accs[slot][:], ACT.Gelu_apprx_tanh, bias=bias[:, m, e : e + 1]
-                    )
+                accs = [psum.tile([P, v - u], F32, name=f"acc{m}_{u}") for u, v in banks]
+                for i in order:
+                    for acc, (u, v) in zip(accs, banks):
+                        for slot in range(u, v, CHUNK):
+                            first = i == order[0] and slot == u
+                            last = i == order[-1] and slot == v - CHUNK
+                            multiply(acc[:, slot - u : slot - u + CHUNK], m, slot, i, first, last)
+                for acc, (u, v) in zip(accs, banks):
+                    for e in range(E):
+                        s0, s1 = max(u, STARTS[e]), min(v, STARTS[e] + COUNTS[e])
+                        if s0 < s1:
+                            nc.scalar.activation(
+                                y[m][:, s0:s1], acc[:, s0 - u : s1 - u], ACT.Gelu_apprx_tanh, bias=bias[:, m, e : e + 1]
+                            )
             for m in range(2):
                 nc.vector.tensor_tensor(
                     result[m][:].indirect(offsets[:, lo // 16 : hi // 16]), y[m][:, lo:hi], gates[:, lo:hi], MULT

@@ -68,9 +68,6 @@ def tile_moe_rag_lin_gelu_kernel(
         for q in range(4):
             src = w8_scales[:, 0, 4 * q : 4 * q + 4, :].bitcast(I32)
             nc.scalar.dma_start(s8[32 * q : 32 * q + 4, :, :].bitcast(I32), src.rearrange("e r n -> r e n"))
-        warm = keep.tile([P, 2], F32, name="warm")
-        nc.vector.memset(warm[:, 0:1], 0.0)
-        nc.scalar.activation(warm[:, 1:2], warm[:, 0:1], ACT.Gelu_apprx_tanh)
 
         raws = {}
         bias = keep.tile([P, 2, E], F32, name="bias")

@@ -15,32 +15,22 @@ MULT = mybir.AluOpType.mult
 
 K, T, E, N = 1536, 1024, 4, 256
 COUNTS = (384, 128, 256, 256)
-STARTS = (0, 384, 512, 768)
+STARTS = (0, 384, 512, 768, 1024)
 P = 128
-CHUNK = 128
 ORDER = (1, 2, 0)
 WIDE = 1408
-RESULT_WIDE = 1280
 FIRST = COUNTS[0]
-PIECES = ((0, FIRST), (FIRST, T))
-PIECE_EXPERTS = ((0, 1), (1, E))
-BANKS = (((0, 384),), ((384, 768), (768, 1024)))
-PASS_ORDER = ((0, 1, 2), (1, 0, 2))
 EARLY = 128
 EARLY_TOKENS = T - COUNTS[0] + EARLY
 LOADS = (
-    ((((512, 448, 0), (256, 0, 0), (256, 96, 0)),),),
-    ((((256, 0, 0), (256, 0, 256)),), (((256, 0, 0), (256, 0, 96)),)),
-    ((((256, 0, 0), (256, 0, 192)),), (((256, 0, 0),),), (((128, 0, 0), (128, 0, 64)),)),
+    (((512, 448, 0), (256, 0, 0), (256, 96, 0)),),
+    (((256, 0, 0), (256, 0, 256)), ((256, 0, 0), (256, 0, 96))),
+    (((256, 0, 0), (256, 0, 192)), ((256, 0, 0),), ((128, 0, 0), (128, 0, 64))),
 )
 TAKES_OVER = {(1, 256): (0, 768), (2, 256): (1, 768), (2, 896): (2, 512)}
 
 FLOPS = 2 * K * N * T
 BYTES = 4 * K * T + E * (512 * N + 1024 * N // 2 + 48 * N) + 4 * N * E + 4 * T + 2 * P * 64 + 4 * N * T
-
-
-def expert_of(slot):
-    return max(e for e in range(E) if STARTS[e] <= slot)
 
 
 def tile_moe_rag_lin_gelu_kernel(
@@ -70,25 +60,13 @@ def tile_moe_rag_lin_gelu_kernel(
             nc.scalar.dma_start(s8[32 * q : 32 * q + 4, :, :].bitcast(I32), src.rearrange("e r n -> r e n"))
 
         raws = {}
-        bias = keep.tile([P, 2, E], F32, name="bias")
         for i, a in enumerate(ORDER):
             rows = xT[512 * a : 512 * (a + 1), :].rearrange("(p j) t -> p j t", j=4)
             lo = 0
-            for steps in LOADS[i]:
-                widths = [sum(unit[0] for unit in units) for units in steps]
-                width = sum(widths)
+            for units in LOADS[i]:
+                width = sum(unit[0] for unit in units)
                 raw = keep.tile([P, 4, width], F32, name=f"raw{i}_{lo}")
-                if len(steps) == 1:
-                    nc.sync.dma_start(raw[:], rows[:, :, lo : lo + width])
-                else:
-                    flat_src = rows.rearrange("p j t -> p (j t)")
-                    flat_dst = raw[:].rearrange("p j t -> p (j t)")
-                    u = 0
-                    v = 3 * T
-                    for step in widths:
-                        v += step
-                        nc.sync.dma_start(flat_dst[:, u:v], flat_src[:, u:v])
-                        u = v
+                nc.sync.dma_start(raw[:], rows[:, :, lo : lo + width])
                 raws[i, lo] = raw
                 if i == 0:
                     nc.sync.dma_start(offsets[:], offs)
@@ -100,9 +78,10 @@ def tile_moe_rag_lin_gelu_kernel(
         w8 = keep.tile([P, E, 4 * N], U8, name="w8", align_bytes=64)
         w4 = keep.tile([P, E, 2, 2 * N], U8, name="w4", align_bytes=64)
         gates = keep.tile([P, T], F32, name="gates")
-        for h, (e0, e1) in enumerate(PIECE_EXPERTS):
+        bias = keep.tile([P, 2, E], F32, name="bias")
+        for e0, e1 in ((0, 1), (1, E)):
             es = slice(e0, e1)
-            g_cols = slice(*PIECES[h])
+            g_cols = slice(STARTS[e0], STARTS[e1])
             nc.sync.dma_start(
                 w4[:, es, :, :].rearrange("p e a x -> p (e a) x").bitcast(I32),
                 w4_words.rearrange("e a p x -> (e a) p x")[2 * e0 : 2 * e1].bitcast(I32).rearrange("g p x -> p g x"),
@@ -111,7 +90,7 @@ def tile_moe_rag_lin_gelu_kernel(
                 w8[:, es, :].bitcast(I32),
                 w8_words[es, 0].rearrange("e p n r -> e p (n r)").bitcast(I32).rearrange("e p x -> p e x"),
             )
-            if h == 0:
+            if e0 == 0:
                 nc.sync.dma_start(bias[:], b.rearrange("(m p) e -> p m e", p=P))
             nc.sync.dma_start(gates[:, g_cols], gate[0:P, g_cols])
 
@@ -128,15 +107,12 @@ def tile_moe_rag_lin_gelu_kernel(
             if gpsimd:
                 u, v = scalar, scalar + gpsimd
                 nc.gpsimd.tensor_copy(grouped[:, u:v, :], raw[:, :, at + u : at + v].rearrange("p j t -> p t j"))
-            for engine, u, v in ((nc.scalar, 0, scalar), (nc.vector, scalar + gpsimd, width)):
-                if u == v:
-                    continue
-                dst = grouped[:, u:v, :].rearrange("p (c i) j -> p c j i", i=4)
-                src = raw[:, :, at + u : at + v].rearrange("p j (c i) -> p c j i", i=4)
-                if engine is nc.scalar:
-                    nc.scalar.copy(dst, src)
-                else:
-                    nc.vector.tensor_copy(dst, src)
+            for copy, u, v in ((nc.scalar.copy, 0, scalar), (nc.vector.tensor_copy, scalar + gpsimd, width)):
+                if u < v:
+                    copy(
+                        grouped[:, u:v, :].rearrange("p (c i) j -> p c j i", i=4),
+                        raw[:, :, at + u : at + v].rearrange("p j (c i) -> p c j i", i=4),
+                    )
             return grouped
 
         def quantize(i, grouped, lo, width):
@@ -146,35 +122,38 @@ def tile_moe_rag_lin_gelu_kernel(
                 in_=grouped[:].rearrange("p t j -> p (t j)"),
             )
 
-        def pick(dst, window, lo, hi):
-            nc.vector.tensor_copy(dst[:, lo:hi], window.indirect(offsets[:, lo // 16 : hi // 16]))
+        def entries(lo, hi):
+            return offsets[:, lo // 16 : hi // 16]
 
-        packed = (bytes_a, None, bytes_bc)
-        picked_packed = (picked_a, None, picked_bc)
+        def pick(dst, window, lo, hi):
+            nc.vector.tensor_copy(dst[:, lo:hi], window.indirect(entries(lo, hi)))
+
         for i in range(3):
             lo = 0
-            for steps in LOADS[i]:
+            for units in LOADS[i]:
                 raw, at = raws[i, lo], 0
-                for units in steps:
-                    ready = []
-                    for width, vector, gpsimd in units:
-                        ready.append((group(i, raw, at, lo, width, vector, gpsimd), lo, width))
-                        at += width
-                        lo += width
-                    for grouped, start, width in ready:
-                        quantize(i, grouped, start, width)
+                ready = []
+                for width, vector, gpsimd in units:
+                    ready.append((group(i, raw, at, lo, width, vector, gpsimd), lo, width))
+                    at += width
+                    lo += width
+                for grouped, start, width in ready:
+                    quantize(i, grouped, start, width)
                 if i == 2 and lo == EARLY_TOKENS:
-                    pick(picked_packed[i], packed[i][:, 0:lo], 0, EARLY)
-                    pick(picked_words[i], words[i][:, 0:lo], 0, EARLY)
-            for u, v in (((0, T),), ((0, T),), ((EARLY, FIRST), (FIRST, T)))[i]:
-                if i != 1:
-                    pick(picked_packed[i], packed[i][:], u, v)
-                pick(picked_words[i], words[i][:], u, v)
+                    pick(picked_bc, bytes_bc[:, 0:lo], 0, EARLY)
+                    pick(picked_words[2], words[2][:, 0:lo], 0, EARLY)
+            if i == 0:
+                pick(picked_a, bytes_a[:], 0, T)
+            if i < 2:
+                pick(picked_words[i], words[i][:], 0, T)
+        pick(picked_bc, bytes_bc[:], EARLY, FIRST)
+        pick(picked_words[2], words[2][:], EARLY, FIRST)
+        pick(picked_bc, bytes_bc[:], FIRST, T)
+        pick(picked_words[2], words[2][:], FIRST, STARTS[3])
+        pick(picked_words[2], words[2][:], STARTS[3], T)
 
-        def multiply(acc, m, slot, i, start, stop):
-            e = expert_of(slot)
+        def multiply(acc, e, m, lo, hi, i, start, stop):
             n_cols = slice(P * m, P * (m + 1))
-            s_cols = slice(slot, slot + CHUNK)
             if i == 2:
                 lhs = w8[:, e, 4 * P * m : 4 * P * (m + 1)].bitcast(FP8X4)
                 lhs_scale = s8[:, e, n_cols]
@@ -185,33 +164,57 @@ def tile_moe_rag_lin_gelu_kernel(
                 out=acc,
                 lhsT=lhs,
                 lhsT_scale=lhs_scale,
-                rhs=picked_words[i][:, s_cols].bitcast(FP8X4),
-                rhs_scale=picked_planes[i][:, s_cols],
+                rhs=picked_words[i][:, lo:hi].bitcast(FP8X4),
+                rhs_scale=picked_planes[i][:, lo:hi],
                 start=start,
                 stop=stop,
             )
 
-        y = [keep.tile([P, T], F32, name=f"y{m}") for m in range(2)]
-        result = [keep.tile([P, RESULT_WIDE], F32, name=f"result{m}") for m in range(2)]
-        for (lo, hi), banks, order in zip(PIECES, BANKS, PASS_ORDER):
-            for m in range(2):
-                accs = [psum.tile([P, v - u], F32, name=f"acc{m}_{u}") for u, v in banks]
-                for i in order:
-                    for acc, (u, v) in zip(accs, banks):
-                        for slot in range(u, v, CHUNK):
-                            first = i == order[0] and slot == u
-                            last = i == order[-1] and slot == v - CHUNK
-                            multiply(acc[:, slot - u : slot - u + CHUNK], m, slot, i, first, last)
-                for acc, (u, v) in zip(accs, banks):
-                    for e in range(E):
-                        s0, s1 = max(u, STARTS[e]), min(v, STARTS[e] + COUNTS[e])
-                        if s0 < s1:
-                            nc.scalar.activation(
-                                y[m][:, s0:s1], acc[:, s0 - u : s1 - u], ACT.Gelu_apprx_tanh, bias=bias[:, m, e : e + 1]
-                            )
-            for m in range(2):
-                nc.vector.tensor_tensor(
-                    result[m][:].indirect(offsets[:, lo // 16 : hi // 16]), y[m][:, lo:hi], gates[:, lo:hi], MULT
-                )
+        def gelu(dst, acc, e, m):
+            nc.scalar.activation(dst, acc, ACT.Gelu_apprx_tanh, bias=bias[:, m, e : e + 1])
+
+        result = [keep.tile([P, T], F32, name=f"result{m}") for m in range(2)]
+
+        def scatter_product(m, y, lo, hi):
+            nc.vector.tensor_tensor(result[m][:].indirect(entries(lo, hi)), y, gates[:, lo:hi], MULT)
+
+        def scatter_copy(m, z, lo, hi):
+            nc.scalar.activation(result[m][:].indirect(entries(lo, hi)), z, ACT.Copy)
+
+        y_first = keep.tile([P, 2, FIRST], F32, name="y_first")
         for m in range(2):
-            nc.sync.dma_start(out[P * m : P * (m + 1), :], result[m][:, 0:T])
+            acc = psum.tile([P, FIRST], F32, name=f"acc_first{m}")
+            for i in range(3):
+                multiply(acc[:, 0:EARLY], 0, m, 0, EARLY, i, i == 0, False)
+                multiply(acc[:, EARLY:FIRST], 0, m, EARLY, FIRST, i, False, i == 2)
+            gelu(y_first[:, m, :], acc[:], 0, m)
+        z_first = keep.tile([P, FIRST], F32, name="shared")
+        half = FIRST // 2
+        for lo in (0, half):
+            nc.gpsimd.tensor_tensor(z_first[:, lo : lo + half], y_first[:, 0, lo : lo + half], gates[:, lo : lo + half], MULT)
+        for lo in (0, half):
+            scatter_copy(0, z_first[:, lo : lo + half], lo, lo + half)
+        scatter_product(1, y_first[:, 1, :], 0, FIRST)
+
+        y_rest = keep.tile([P, 2, T - FIRST], F32, name="shared")
+        banks = (((1, 0), (1, 1)), ((2, 1),), ((2, 0),), ((3, 0),), ((3, 1),))
+        accs = [psum.tile([P, len(sums), COUNTS[sums[0][0]]], F32, name=f"acc{n}") for n, sums in enumerate(banks)]
+        for i in range(3):
+            for acc, sums in zip(accs, banks):
+                for s, (e, m) in enumerate(sums):
+                    multiply(acc[:, s, :], e, m, STARTS[e], STARTS[e + 1], i, i == 0 and s == 0, i == 2 and s == len(sums) - 1)
+
+        def y_of(m, lo, hi):
+            return y_rest[:, m, lo - FIRST : hi - FIRST]
+
+        for acc, sums in zip(accs, banks):
+            for s, (e, m) in enumerate(sums):
+                gelu(y_of(m, STARTS[e], STARTS[e + 1]), acc[:, s, :], e, m)
+        z_rest = keep.tile([P, STARTS[3] - FIRST], F32, name="z_rest")
+        scatter_product(0, y_of(0, FIRST, STARTS[2]), FIRST, STARTS[2])
+        nc.vector.tensor_tensor(z_rest[:], y_of(1, FIRST, STARTS[3]), gates[:, FIRST : STARTS[3]], MULT)
+        scatter_copy(1, z_rest[:], FIRST, STARTS[3])
+        for e, m in ((2, 0), (3, 0), (3, 1)):
+            scatter_product(m, y_of(m, STARTS[e], STARTS[e + 1]), STARTS[e], STARTS[e + 1])
+        for m in range(2):
+            nc.sync.dma_start(out[P * m : P * (m + 1), :], result[m][:])

@@ -1,6 +1,7 @@
 from contextlib import ExitStack
 
 import concourse.mybir as mybir
+from concourse.masks import make_identity
 
 F32 = mybir.dt.float32
 BF16 = mybir.dt.bfloat16
@@ -43,6 +44,9 @@ def tile_moe_rag_lin_gelu_kernel(
 
         offsets = keep.tile([P, T // 16], U16, name="offsets")
 
+        gate_row = keep.tile([P, 8], F32, name="gate_row")
+        nc.sync.dma_start(gate_row[:], gate[0].rearrange("(q c) -> q c", c=8))
+
         bytes_a = keep.tile([P, WIDE], U8, name="bytes_a", align_bytes=64)
         bytes_bc = keep.tile([P, T], U8, name="bytes_bc", align_bytes=64)
         s8 = keep.tile([P, E, N], U8, name="s8", align_bytes=64)
@@ -58,6 +62,18 @@ def tile_moe_rag_lin_gelu_kernel(
         for q in range(4):
             src = w8_scales[:, 0, 4 * q : 4 * q + 4, :].bitcast(I32)
             nc.scalar.dma_start(s8[32 * q : 32 * q + 4, :, :].bitcast(I32), src.rearrange("e r n -> r e n"))
+
+        identity = keep.tile([P, P], F32, name="identity")
+        make_identity(nc, identity[:])
+        gates = keep.tile([P, T], F32, name="gates")
+        for h in range(2):
+            spread = psum.tile([P, 4, P], F32, name=f"acc_first{h}")
+            for c in range(4):
+                column = gate_row[:, 4 * h + c : 4 * h + c + 1]
+                nc.tensor.transpose(spread[:, c, :], column.to_broadcast([P, P]), identity[:])
+            nc.scalar.copy(
+                gates[:].rearrange("p (q h c) -> p q h c", h=2, c=4)[:, :, h, :], spread[:].rearrange("p c q -> p q c")
+            )
 
         raws = {}
         for i, a in enumerate(ORDER):
@@ -77,11 +93,9 @@ def tile_moe_rag_lin_gelu_kernel(
             nc.sync.dma_start(s4[32 * q : 32 * q + 4, :, :].bitcast(I32), src.rearrange("g r n -> r g n"))
         w8 = keep.tile([P, E, 4 * N], U8, name="w8", align_bytes=64)
         w4 = keep.tile([P, E, 2, 2 * N], U8, name="w4", align_bytes=64)
-        gates = keep.tile([P, T], F32, name="gates")
         bias = keep.tile([P, 2, E], F32, name="bias")
-        for e0, e1 in ((0, 1), (1, E)):
+        for e0, e1 in ((0, 1), (1, 3), (3, E)):
             es = slice(e0, e1)
-            g_cols = slice(STARTS[e0], STARTS[e1])
             nc.sync.dma_start(
                 w4[:, es, :, :].rearrange("p e a x -> p (e a) x").bitcast(I32),
                 w4_words.rearrange("e a p x -> (e a) p x")[2 * e0 : 2 * e1].bitcast(I32).rearrange("g p x -> p g x"),
@@ -92,7 +106,6 @@ def tile_moe_rag_lin_gelu_kernel(
             )
             if e0 == 0:
                 nc.sync.dma_start(bias[:], b.rearrange("(m p) e -> p m e", p=P))
-            nc.sync.dma_start(gates[:, g_cols], gate[0:P, g_cols])
 
         picked_a = keep.tile([P, T], U8, name="picked_a", align_bytes=64)
         picked_bc = keep.tile([P, T], U8, name="picked_bc", align_bytes=64)
@@ -189,11 +202,8 @@ def tile_moe_rag_lin_gelu_kernel(
                 multiply(acc[:, EARLY:FIRST], 0, m, EARLY, FIRST, i, False, i == 2)
             gelu(y_first[:, m, :], acc[:], 0, m)
         z_first = keep.tile([P, FIRST], F32, name="shared")
-        half = FIRST // 2
-        for lo in (0, half):
-            nc.gpsimd.tensor_tensor(z_first[:, lo : lo + half], y_first[:, 0, lo : lo + half], gates[:, lo : lo + half], MULT)
-        for lo in (0, half):
-            scatter_copy(0, z_first[:, lo : lo + half], lo, lo + half)
+        nc.vector.tensor_tensor(z_first[:], y_first[:, 0, :], gates[:, 0:FIRST], MULT)
+        scatter_copy(0, z_first[:], 0, FIRST)
         scatter_product(1, y_first[:, 1, :], 0, FIRST)
 
         y_rest = keep.tile([P, 2, T - FIRST], F32, name="shared")

@@ -94,7 +94,7 @@ def tile_moe_rag_lin_gelu_kernel(
         w8 = keep.tile([P, E, 4 * N], U8, name="w8", align_bytes=64)
         w4 = keep.tile([P, E, 2, 2 * N], U8, name="w4", align_bytes=64)
         bias = keep.tile([P, 2, E], F32, name="bias")
-        for e0, e1 in ((0, 1), (1, 3), (3, E)):
+        for e0, e1 in ((0, 1), (1, E)):
             es = slice(e0, e1)
             nc.sync.dma_start(
                 w4[:, es, :, :].rearrange("p e a x -> p (e a) x").bitcast(I32),
@@ -186,13 +186,16 @@ def tile_moe_rag_lin_gelu_kernel(
         def gelu(dst, acc, e, m):
             nc.scalar.activation(dst, acc, ACT.Gelu_apprx_tanh, bias=bias[:, m, e : e + 1])
 
-        result = [keep.tile([P, T], F32, name=f"result{m}") for m in range(2)]
-
         def scatter_product(m, y, lo, hi):
             nc.vector.tensor_tensor(result[m][:].indirect(entries(lo, hi)), y, gates[:, lo:hi], MULT)
 
         def scatter_copy(m, z, lo, hi):
             nc.scalar.activation(result[m][:].indirect(entries(lo, hi)), z, ACT.Copy)
+
+        def product(dst, y, lo, hi):
+            blocks = dst.shape[1]
+            weights = gates[:, lo:hi].unsqueeze(1).to_broadcast([P, blocks, hi - lo])
+            nc.vector.tensor_tensor(dst, y, weights, MULT)
 
         y_first = keep.tile([P, 2, FIRST], F32, name="y_first")
         for m in range(2):
@@ -201,30 +204,30 @@ def tile_moe_rag_lin_gelu_kernel(
                 multiply(acc[:, 0:EARLY], 0, m, 0, EARLY, i, i == 0, False)
                 multiply(acc[:, EARLY:FIRST], 0, m, EARLY, FIRST, i, False, i == 2)
             gelu(y_first[:, m, :], acc[:], 0, m)
-        z_first = keep.tile([P, FIRST], F32, name="shared")
-        nc.vector.tensor_tensor(z_first[:], y_first[:, 0, :], gates[:, 0:FIRST], MULT)
-        scatter_copy(0, z_first[:], 0, FIRST)
-        scatter_product(1, y_first[:, 1, :], 0, FIRST)
 
-        y_rest = keep.tile([P, 2, T - FIRST], F32, name="shared")
         banks = (((1, 0), (1, 1)), ((2, 1),), ((2, 0),), ((3, 0),), ((3, 1),))
         accs = [psum.tile([P, len(sums), COUNTS[sums[0][0]]], F32, name=f"acc{n}") for n, sums in enumerate(banks)]
         for i in range(3):
             for acc, sums in zip(accs, banks):
                 for s, (e, m) in enumerate(sums):
                     multiply(acc[:, s, :], e, m, STARTS[e], STARTS[e + 1], i, i == 0 and s == 0, i == 2 and s == len(sums) - 1)
-
-        def y_of(m, lo, hi):
-            return y_rest[:, m, lo - FIRST : hi - FIRST]
-
+        y = {e: keep.tile([P, 2, COUNTS[e]], F32, name=f"y{e}") for e in range(1, E)}
         for acc, sums in zip(accs, banks):
             for s, (e, m) in enumerate(sums):
-                gelu(y_of(m, STARTS[e], STARTS[e + 1]), acc[:, s, :], e, m)
-        z_rest = keep.tile([P, STARTS[3] - FIRST], F32, name="z_rest")
-        scatter_product(0, y_of(0, FIRST, STARTS[2]), FIRST, STARTS[2])
-        nc.vector.tensor_tensor(z_rest[:], y_of(1, FIRST, STARTS[3]), gates[:, FIRST : STARTS[3]], MULT)
-        scatter_copy(1, z_rest[:], FIRST, STARTS[3])
+                gelu(y[e][:, m, :], acc[:, s, :], e, m)
+
+        result = [keep.tile([P, T], F32, name="result0")]
+        scatter_product(0, y_first[:, 0, :], 0, FIRST)
+        z1 = keep.tile([P, 2, COUNTS[1]], F32, name="z1")
+        product(z1[:], y[1][:], STARTS[1], STARTS[2])
+        result.append(keep.tile([P, T], F32, name="y1"))
+        scatter_product(1, y_first[:, 1, :], 0, FIRST)
+        z2 = keep.tile([P, 1, COUNTS[2]], F32, name="z2")
+        product(z2[:], y[2][:, 1:2, :], STARTS[2], STARTS[3])
+        for m in range(2):
+            scatter_copy(m, z1[:, m, :], STARTS[1], STARTS[2])
+        scatter_copy(1, z2[:, 0, :], STARTS[2], STARTS[3])
         for e, m in ((2, 0), (3, 0), (3, 1)):
-            scatter_product(m, y_of(m, STARTS[e], STARTS[e + 1]), STARTS[e], STARTS[e + 1])
+            scatter_product(m, y[e][:, m, :], STARTS[e], STARTS[e + 1])
         for m in range(2):
             nc.sync.dma_start(out[P * m : P * (m + 1), :], result[m][:])

@@ -192,11 +192,6 @@ def tile_moe_rag_lin_gelu_kernel(
         def scatter_copy(m, z, lo, hi):
             nc.scalar.activation(result[m][:].indirect(entries(lo, hi)), z, ACT.Copy)
 
-        def product(dst, y, lo, hi):
-            blocks = dst.shape[1]
-            weights = gates[:, lo:hi].unsqueeze(1).to_broadcast([P, blocks, hi - lo])
-            nc.vector.tensor_tensor(dst, y, weights, MULT)
-
         y_first = keep.tile([P, 2, FIRST], F32, name="y_first")
         for m in range(2):
             acc = psum.tile([P, FIRST], F32, name=f"acc_first{m}")
@@ -205,29 +200,36 @@ def tile_moe_rag_lin_gelu_kernel(
                 multiply(acc[:, EARLY:FIRST], 0, m, EARLY, FIRST, i, False, i == 2)
             gelu(y_first[:, m, :], acc[:], 0, m)
 
-        banks = (((1, 0), (1, 1)), ((2, 1),), ((2, 0),), ((3, 0),), ((3, 1),))
-        accs = [psum.tile([P, len(sums), COUNTS[sums[0][0]]], F32, name=f"acc{n}") for n, sums in enumerate(banks)]
+        banks = (((1, 0), (2, 0)), ((1, 1), (2, 1)), ((3, 1),), ((3, 0),))
+        accs = {}
+        for n, sums in enumerate(banks):
+            base = STARTS[sums[0][0]]
+            bank = psum.tile([P, STARTS[sums[-1][0] + 1] - base], F32, name=f"acc{n}")
+            for e, m in sums:
+                accs[e, m] = bank[:, STARTS[e] - base : STARTS[e + 1] - base]
         for i in range(3):
-            for acc, sums in zip(accs, banks):
-                for s, (e, m) in enumerate(sums):
-                    multiply(acc[:, s, :], e, m, STARTS[e], STARTS[e + 1], i, i == 0 and s == 0, i == 2 and s == len(sums) - 1)
-        y = {e: keep.tile([P, 2, COUNTS[e]], F32, name=f"y{e}") for e in range(1, E)}
-        for acc, sums in zip(accs, banks):
-            for s, (e, m) in enumerate(sums):
-                gelu(y[e][:, m, :], acc[:, s, :], e, m)
+            for sums in banks:
+                for e, m in sums:
+                    start = i == 0 and (e, m) == sums[0]
+                    stop = i == 2 and (e, m) == sums[-1]
+                    multiply(accs[e, m], e, m, STARTS[e], STARTS[e + 1], i, start, stop)
+        y_rest = keep.tile([P, 2, T - FIRST], F32, name="y_rest")
 
-        result = [keep.tile([P, T], F32, name="result0")]
-        scatter_product(0, y_first[:, 0, :], 0, FIRST)
-        z1 = keep.tile([P, 2, COUNTS[1]], F32, name="z1")
-        product(z1[:], y[1][:], STARTS[1], STARTS[2])
-        result.append(keep.tile([P, T], F32, name="y1"))
-        scatter_product(1, y_first[:, 1, :], 0, FIRST)
-        z2 = keep.tile([P, 1, COUNTS[2]], F32, name="z2")
-        product(z2[:], y[2][:, 1:2, :], STARTS[2], STARTS[3])
+        def y_of(m, lo, hi):
+            return y_rest[:, m, lo - FIRST : hi - FIRST]
+
+        for sums in banks:
+            for e, m in sums:
+                gelu(y_of(m, STARTS[e], STARTS[e + 1]), accs[e, m], e, m)
+
+        result = [keep.tile([P, T], F32, name=f"result{m}") for m in range(2)]
         for m in range(2):
-            scatter_copy(m, z1[:, m, :], STARTS[1], STARTS[2])
-        scatter_copy(1, z2[:, 0, :], STARTS[2], STARTS[3])
-        for e, m in ((2, 0), (3, 0), (3, 1)):
-            scatter_product(m, y[e][:, m, :], STARTS[e], STARTS[e + 1])
-        for m in range(2):
+            scatter_product(m, y_first[:, m, :], 0, FIRST)
+        z = keep.tile([P, STARTS[3] - FIRST], F32, name="z")
+        nc.vector.tensor_tensor(z[:], y_of(0, FIRST, STARTS[3]), gates[:, FIRST : STARTS[3]], MULT)
+        scatter_copy(0, z[:], FIRST, STARTS[3])
+        scatter_product(1, y_of(1, FIRST, STARTS[3]), FIRST, STARTS[3])
+        for m in (1, 0):
+            scatter_product(m, y_of(m, STARTS[3], T), STARTS[3], T)
+        for m in (1, 0):
             nc.sync.dma_start(out[P * m : P * (m + 1), :], result[m][:])

@@ -192,13 +192,18 @@ def tile_moe_rag_lin_gelu_kernel(
         def scatter_copy(m, z, lo, hi):
             nc.scalar.activation(result[m][:].indirect(entries(lo, hi)), z, ACT.Copy)
 
+        result = [keep.tile([P, T], F32, name=f"result{m}") for m in range(2)]
         y_first = keep.tile([P, 2, FIRST], F32, name="y_first")
+        z_early = keep.tile([P, 2, EARLY], F32, name="z_early")
+        for lo, hi in ((0, EARLY), (EARLY, FIRST)):
+            for m in range(2):
+                acc = psum.tile([P, hi - lo], F32, name=f"acc_first{m}" if lo else f"acc_early{m}")
+                for i in range(3):
+                    multiply(acc[:], 0, m, lo, hi, i, i == 0, i == 2)
+                gelu(y_first[:, m, lo:hi], acc[:], 0, m)
         for m in range(2):
-            acc = psum.tile([P, FIRST], F32, name=f"acc_first{m}")
-            for i in range(3):
-                multiply(acc[:, 0:EARLY], 0, m, 0, EARLY, i, i == 0, False)
-                multiply(acc[:, EARLY:FIRST], 0, m, EARLY, FIRST, i, False, i == 2)
-            gelu(y_first[:, m, :], acc[:], 0, m)
+            nc.gpsimd.tensor_tensor(z_early[:, m, :], y_first[:, m, 0:EARLY], gates[:, 0:EARLY], MULT)
+            scatter_copy(m, z_early[:, m, :], 0, EARLY)
 
         banks = (((1, 0), (2, 0)), ((1, 1), (2, 1)), ((3, 1),), ((3, 0),))
         accs = {}
@@ -222,9 +227,8 @@ def tile_moe_rag_lin_gelu_kernel(
             for e, m in sums:
                 gelu(y_of(m, STARTS[e], STARTS[e + 1]), accs[e, m], e, m)
 
-        result = [keep.tile([P, T], F32, name=f"result{m}") for m in range(2)]
         for m in range(2):
-            scatter_product(m, y_first[:, m, :], 0, FIRST)
+            scatter_product(m, y_first[:, m, EARLY:FIRST], EARLY, FIRST)
         z = keep.tile([P, STARTS[3] - FIRST], F32, name="z")
         nc.vector.tensor_tensor(z[:], y_of(0, FIRST, STARTS[3]), gates[:, FIRST : STARTS[3]], MULT)
         scatter_copy(0, z[:], FIRST, STARTS[3])

@@ -63,6 +63,10 @@ def tile_moe_rag_lin_gelu_kernel(
             src = w8_scales[:, 0, 4 * q : 4 * q + 4, :].bitcast(I32)
             nc.scalar.dma_start(s8[32 * q : 32 * q + 4, :, :].bitcast(I32), src.rearrange("e r n -> r e n"))
 
+        warm = keep.tile([P, 2], F32, name="warm")
+        nc.vector.memset(warm[:, 0:1], 0.0)
+        nc.scalar.activation(warm[:, 1:2], warm[:, 0:1], ACT.Gelu_apprx_tanh)
+
         identity = keep.tile([P, P], F32, name="identity")
         make_identity(nc, identity[:])
         gates = keep.tile([P, T], F32, name="gates")
@@ -193,17 +197,22 @@ def tile_moe_rag_lin_gelu_kernel(
             nc.scalar.activation(result[m][:].indirect(entries(lo, hi)), z, ACT.Copy)
 
         result = [keep.tile([P, T], F32, name=f"result{m}") for m in range(2)]
-        y_first = keep.tile([P, 2, FIRST], F32, name="y_first")
-        z_early = keep.tile([P, 2, EARLY], F32, name="z_early")
-        for lo, hi in ((0, EARLY), (EARLY, FIRST)):
+
+        def first_expert(y, lo, hi):
             for m in range(2):
-                acc = psum.tile([P, hi - lo], F32, name=f"acc_first{m}" if lo else f"acc_early{m}")
+                acc = psum.tile([P, hi - lo], F32, name=f"acc_first{m}")
                 for i in range(3):
                     multiply(acc[:], 0, m, lo, hi, i, i == 0, i == 2)
-                gelu(y_first[:, m, lo:hi], acc[:], 0, m)
+                gelu(y[:, m, 0 : hi - lo], acc[:], 0, m)
+
+        y_early = keep.tile([P, 2, EARLY], F32, name="y_early")
+        first_expert(y_early, 0, EARLY)
+        z_early = keep.tile([P, 2, EARLY], F32, name="shared")
         for m in range(2):
-            nc.gpsimd.tensor_tensor(z_early[:, m, :], y_first[:, m, 0:EARLY], gates[:, 0:EARLY], MULT)
+            nc.gpsimd.tensor_tensor(z_early[:, m, :], y_early[:, m, :], gates[:, 0:EARLY], MULT)
             scatter_copy(m, z_early[:, m, :], 0, EARLY)
+        y_rest = keep.tile([P, 2, T - EARLY], F32, name="shared")
+        first_expert(y_rest, EARLY, FIRST)
 
         banks = (((1, 0), (2, 0)), ((1, 1), (2, 1)), ((3, 1),), ((3, 0),))
         accs = {}
@@ -212,23 +221,22 @@ def tile_moe_rag_lin_gelu_kernel(
             bank = psum.tile([P, STARTS[sums[-1][0] + 1] - base], F32, name=f"acc{n}")
             for e, m in sums:
                 accs[e, m] = bank[:, STARTS[e] - base : STARTS[e + 1] - base]
-        for i in range(3):
-            for sums in banks:
+        for sums in banks:
+            for i in (1, 0, 2):
                 for e, m in sums:
-                    start = i == 0 and (e, m) == sums[0]
+                    start = i == 1 and (e, m) == sums[0]
                     stop = i == 2 and (e, m) == sums[-1]
                     multiply(accs[e, m], e, m, STARTS[e], STARTS[e + 1], i, start, stop)
-        y_rest = keep.tile([P, 2, T - FIRST], F32, name="y_rest")
 
         def y_of(m, lo, hi):
-            return y_rest[:, m, lo - FIRST : hi - FIRST]
+            return y_rest[:, m, lo - EARLY : hi - EARLY]
 
         for sums in banks:
             for e, m in sums:
                 gelu(y_of(m, STARTS[e], STARTS[e + 1]), accs[e, m], e, m)
 
         for m in range(2):
-            scatter_product(m, y_first[:, m, EARLY:FIRST], EARLY, FIRST)
+            scatter_product(m, y_of(m, EARLY, FIRST), EARLY, FIRST)
         z = keep.tile([P, STARTS[3] - FIRST], F32, name="z")
         nc.vector.tensor_tensor(z[:], y_of(0, FIRST, STARTS[3]), gates[:, FIRST : STARTS[3]], MULT)
         scatter_copy(0, z[:], FIRST, STARTS[3])

@@ -198,29 +198,29 @@ def tile_moe_rag_lin_gelu_kernel(
 
         result = [keep.tile([P, T], F32, name=f"result{m}") for m in range(2)]
 
-        def first_expert(y, lo, hi):
-            for m in range(2):
-                acc = psum.tile([P, hi - lo], F32, name=f"acc_first{m}")
-                for i in range(3):
-                    multiply(acc[:], 0, m, lo, hi, i, i == 0, i == 2)
-                gelu(y[:, m, 0 : hi - lo], acc[:], 0, m)
+        def first_expert(y, m, lo, hi):
+            acc = psum.tile([P, hi - lo], F32, name=f"acc_first{m}")
+            for i in range(3):
+                multiply(acc[:], 0, m, lo, hi, i, i == 0, i == 2)
+            gelu(y, acc[:], 0, m)
 
         y_early = keep.tile([P, 2, EARLY], F32, name="y_early")
-        first_expert(y_early, 0, EARLY)
-        z_early = keep.tile([P, 2, EARLY], F32, name="shared")
         for m in range(2):
-            nc.gpsimd.tensor_tensor(z_early[:, m, :], y_early[:, m, :], gates[:, 0:EARLY], MULT)
-            scatter_copy(m, z_early[:, m, :], 0, EARLY)
-        y_rest = keep.tile([P, 2, T - EARLY], F32, name="shared")
-        first_expert(y_rest, EARLY, FIRST)
+            first_expert(y_early[:, m, :], m, 0, EARLY)
+        y_rest = []
+        for m in range(2):
+            z_early = keep.tile([P, EARLY], F32, name=f"shared{m}")
+            nc.gpsimd.tensor_tensor(z_early[:], y_early[:, m, :], gates[:, 0:EARLY], MULT)
+            scatter_copy(m, z_early[:], 0, EARLY)
+            y_rest.append(keep.tile([P, T - EARLY], F32, name=f"shared{m}"))
+            first_expert(y_rest[m][:, 0 : FIRST - EARLY], m, EARLY, FIRST)
 
-        banks = (((1, 0), (2, 0)), ((1, 1), (2, 1)), ((3, 1),), ((3, 0),))
+        banks = (((1, 1), (1, 0)), ((2, 0),), ((2, 1),), ((3, 1),), ((3, 0),))
         accs = {}
         for n, sums in enumerate(banks):
-            base = STARTS[sums[0][0]]
-            bank = psum.tile([P, STARTS[sums[-1][0] + 1] - base], F32, name=f"acc{n}")
-            for e, m in sums:
-                accs[e, m] = bank[:, STARTS[e] - base : STARTS[e + 1] - base]
+            bank = psum.tile([P, len(sums), COUNTS[sums[0][0]]], F32, name=f"acc{n}")
+            for place, key in enumerate(sums):
+                accs[key] = bank[:, place, :]
         for sums in banks:
             for i in (1, 0, 2):
                 for e, m in sums:
@@ -229,19 +229,18 @@ def tile_moe_rag_lin_gelu_kernel(
                     multiply(accs[e, m], e, m, STARTS[e], STARTS[e + 1], i, start, stop)
 
         def y_of(m, lo, hi):
-            return y_rest[:, m, lo - EARLY : hi - EARLY]
+            return y_rest[m][:, lo - EARLY : hi - EARLY]
 
         for sums in banks:
             for e, m in sums:
                 gelu(y_of(m, STARTS[e], STARTS[e + 1]), accs[e, m], e, m)
 
-        for m in range(2):
-            scatter_product(m, y_of(m, EARLY, FIRST), EARLY, FIRST)
+        for m, hi in ((0, FIRST), (1, STARTS[2])):
+            scatter_product(m, y_of(m, EARLY, hi), EARLY, hi)
         z = keep.tile([P, STARTS[3] - FIRST], F32, name="z")
         nc.vector.tensor_tensor(z[:], y_of(0, FIRST, STARTS[3]), gates[:, FIRST : STARTS[3]], MULT)
         scatter_copy(0, z[:], FIRST, STARTS[3])
-        scatter_product(1, y_of(1, FIRST, STARTS[3]), FIRST, STARTS[3])
-        for m in (1, 0):
-            scatter_product(m, y_of(m, STARTS[3], T), STARTS[3], T)
+        for m, lo in ((1, STARTS[2]), (0, STARTS[3])):
+            scatter_product(m, y_of(m, lo, T), lo, T)
         for m in (1, 0):
             nc.sync.dma_start(out[P * m : P * (m + 1), :], result[m][:])

@@ -24,10 +24,11 @@ FIRST = COUNTS[0]
 EARLY = 128
 EARLY_TOKENS = T - COUNTS[0] + EARLY
 LOADS = (
-    (((512, 448, 0), (256, 0, 0), (256, 96, 0)),),
+    (((512, 320, 0), (256, 224, 0), (256, 0, 0)),),
     (((256, 0, 0), (256, 0, 256)), ((256, 0, 0), (256, 0, 96))),
     (((256, 0, 0), (256, 0, 192)), ((256, 0, 0),), ((128, 0, 0), (128, 0, 64))),
 )
+STEPS = (512, 1024)
 TAKES_OVER = {(1, 256): (0, 768), (2, 256): (1, 768), (2, 896): (2, 512)}
 
 FLOPS = 2 * K * N * T
@@ -86,7 +87,14 @@ def tile_moe_rag_lin_gelu_kernel(
             for units in LOADS[i]:
                 width = sum(unit[0] for unit in units)
                 raw = keep.tile([P, 4, width], F32, name=f"raw{i}_{lo}")
-                nc.sync.dma_start(raw[:], rows[:, :, lo : lo + width])
+                if i == 0:
+                    flat_src = rows.rearrange("p j t -> p (j t)")
+                    flat_dst = raw[:].rearrange("p j t -> p (j t)")
+                    ends = [3 * T + tokens for tokens in STEPS]
+                    for u, v in zip([0] + ends, ends):
+                        nc.sync.dma_start(flat_dst[:, u:v], flat_src[:, u:v])
+                else:
+                    nc.sync.dma_start(raw[:], rows[:, :, lo : lo + width])
                 raws[i, lo] = raw
                 if i == 0:
                     nc.sync.dma_start(offsets[:], offs)

from contextlib import ExitStack

import concourse.mybir as mybir
from concourse.masks import make_identity

F32 = mybir.dt.float32
BF16 = mybir.dt.bfloat16
I32 = mybir.dt.int32
U32 = mybir.dt.uint32
U16 = mybir.dt.uint16
U8 = mybir.dt.uint8
FP8X4 = mybir.dt.float8_e4m3fn_x4
FP4X4 = mybir.dt.float4_e2m1fn_x4
ACT = mybir.ActivationFunctionType
MULT = mybir.AluOpType.mult

K, T, E, N = 1536, 1024, 4, 256
COUNTS = (384, 128, 256, 256)
STARTS = (0, 384, 512, 768, 1024)
P = 128
ORDER = (1, 2, 0)
WIDE = 1408
FIRST = COUNTS[0]
EARLY = 128
EARLY_TOKENS = T - COUNTS[0] + EARLY
LOADS = (
    (((512, 320, 0), (256, 224, 0), (256, 0, 0)),),
    (((256, 0, 0), (256, 0, 256)), ((256, 0, 0), (256, 0, 96))),
    (((256, 0, 0), (256, 0, 192)), ((256, 0, 0),), ((128, 0, 0), (128, 0, 64))),
)
STEPS = (512, 1024)
TAKES_OVER = {(1, 256): (0, 768), (2, 256): (1, 768), (2, 896): (2, 512)}

FLOPS = 2 * K * N * T
BYTES = 4 * K * T + E * (512 * N + 1024 * N // 2 + 48 * N) + 4 * N * E + 4 * T + 2 * P * 64 + 4 * N * T


def tile_moe_rag_lin_gelu_kernel(
    tc, xT, w8_words, w8_scales, w4_words, w4_scales, b, gate, offs, out
):
    nc = tc.nc
    with ExitStack() as ctx:
        keep = ctx.enter_context(tc.tile_pool(name="keep", bufs=1))
        psum = ctx.enter_context(tc.psum_pool(name="psum", bufs=1))

        offsets = keep.tile([P, T // 16], U16, name="offsets")

        gate_row = keep.tile([P, 8], F32, name="gate_row")
        nc.sync.dma_start(gate_row[:], gate[0].rearrange("(q c) -> q c", c=8))

        bytes_a = keep.tile([P, WIDE], U8, name="bytes_a", align_bytes=64)
        bytes_bc = keep.tile([P, T], U8, name="bytes_bc", align_bytes=64)
        s8 = keep.tile([P, E, N], U8, name="s8", align_bytes=64)
        s4 = keep.tile([P, 2 * E, N], U8, name="s4", align_bytes=64)
        words = [keep.tile([P, WIDE if i < 2 else T], U32, name=f"words{i}", align_bytes=64) for i in range(3)]
        nc.gpsimd.memset(s8[:].rearrange("p e n -> p (e n)").bitcast(I32), 0)
        nc.gpsimd.memset(s4[:].rearrange("p e n -> p (e n)").bitcast(I32), 0)
        nc.gpsimd.memset(bytes_a[:].bitcast(I32), 0)
        nc.gpsimd.memset(words[0][:, T:WIDE].bitcast(I32), 0)
        nc.gpsimd.memset(bytes_bc[:].bitcast(I32), 0)
        nc.gpsimd.memset(words[1][:, T:WIDE].bitcast(I32), 0)

        for q in range(4):
            src = w8_scales[:, 0, 4 * q : 4 * q + 4, :].bitcast(I32)
            nc.scalar.dma_start(s8[32 * q : 32 * q + 4, :, :].bitcast(I32), src.rearrange("e r n -> r e n"))

        warm = keep.tile([P, 2], F32, name="warm")
        nc.vector.memset(warm[:, 0:1], 0.0)
        nc.scalar.activation(warm[:, 1:2], warm[:, 0:1], ACT.Gelu_apprx_tanh)

        identity = keep.tile([P, P], F32, name="identity")
        make_identity(nc, identity[:])
        gates = keep.tile([P, T], F32, name="gates")
        for h in range(2):
            spread = psum.tile([P, 4, P], F32, name=f"acc_first{h}")
            for c in range(4):
                column = gate_row[:, 4 * h + c : 4 * h + c + 1]
                nc.tensor.transpose(spread[:, c, :], column.to_broadcast([P, P]), identity[:])
            nc.scalar.copy(
                gates[:].rearrange("p (q h c) -> p q h c", h=2, c=4)[:, :, h, :], spread[:].rearrange("p c q -> p q c")
            )

        raws = {}
        for i, a in enumerate(ORDER):
            rows = xT[512 * a : 512 * (a + 1), :].rearrange("(p j) t -> p j t", j=4)
            lo = 0
            for units in LOADS[i]:
                width = sum(unit[0] for unit in units)
                raw = keep.tile([P, 4, width], F32, name=f"raw{i}_{lo}")
                if i == 0:
                    flat_src = rows.rearrange("p j t -> p (j t)")
                    flat_dst = raw[:].rearrange("p j t -> p (j t)")
                    ends = [3 * T + tokens for tokens in STEPS]
                    for u, v in zip([0] + ends, ends):
                        nc.sync.dma_start(flat_dst[:, u:v], flat_src[:, u:v])
                else:
                    nc.sync.dma_start(raw[:], rows[:, :, lo : lo + width])
                raws[i, lo] = raw
                if i == 0:
                    nc.sync.dma_start(offsets[:], offs)
                lo += width
        w4s = w4_scales.rearrange("e a q n -> (e a) q n")
        for q in range(4):
            src = w4s[:, 4 * q : 4 * q + 4, :].bitcast(I32)
            nc.sync.dma_start(s4[32 * q : 32 * q + 4, :, :].bitcast(I32), src.rearrange("g r n -> r g n"))
        w8 = keep.tile([P, E, 4 * N], U8, name="w8", align_bytes=64)
        w4 = keep.tile([P, E, 2, 2 * N], U8, name="w4", align_bytes=64)
        bias = keep.tile([P, 2, E], F32, name="bias")
        for e0, e1 in ((0, 1), (1, E)):
            es = slice(e0, e1)
            nc.sync.dma_start(
                w4[:, es, :, :].rearrange("p e a x -> p (e a) x").bitcast(I32),
                w4_words.rearrange("e a p x -> (e a) p x")[2 * e0 : 2 * e1].bitcast(I32).rearrange("g p x -> p g x"),
            )
            nc.sync.dma_start(
                w8[:, es, :].bitcast(I32),
                w8_words[es, 0].rearrange("e p n r -> e p (n r)").bitcast(I32).rearrange("e p x -> p e x"),
            )
            if e0 == 0:
                nc.sync.dma_start(bias[:], b.rearrange("(m p) e -> p m e", p=P))

        picked_a = keep.tile([P, T], U8, name="picked_a", align_bytes=64)
        picked_bc = keep.tile([P, T], U8, name="picked_bc", align_bytes=64)
        planes = (bytes_a[:], bytes_bc[:], bytes_bc[4:P, :])
        picked_planes = (picked_a[:], picked_bc[:], picked_bc[4:P, :])
        picked_words = [keep.tile([P, T], U32, name=f"picked_words{i}", align_bytes=64) for i in range(3)]

        def group(i, raw, at, lo, width, vector, gpsimd):
            owner = TAKES_OVER.get((i, lo), (i, lo))
            grouped = keep.tile([P, width, 4], BF16, name=f"grouped{owner[0]}_{owner[1]}", align_bytes=64)
            scalar = width - vector - gpsimd
            if gpsimd:
                u, v = scalar, scalar + gpsimd
                nc.gpsimd.tensor_copy(grouped[:, u:v, :], raw[:, :, at + u : at + v].rearrange("p j t -> p t j"))
            for copy, u, v in ((nc.scalar.copy, 0, scalar), (nc.vector.tensor_copy, scalar + gpsimd, width)):
                if u < v:
                    copy(
                        grouped[:, u:v, :].rearrange("p (c i) j -> p c j i", i=4),
                        raw[:, :, at + u : at + v].rearrange("p j (c i) -> p c j i", i=4),
                    )
            return grouped

        def quantize(i, grouped, lo, width):
            nc.vector.quantize_mx(
                out=words[i][:, lo : lo + width].bitcast(FP8X4),
                scales=planes[i][:, lo : lo + width],
                in_=grouped[:].rearrange("p t j -> p (t j)"),
            )

        def entries(lo, hi):
            return offsets[:, lo // 16 : hi // 16]

        def pick(dst, window, lo, hi):
            nc.vector.tensor_copy(dst[:, lo:hi], window.indirect(entries(lo, hi)))

        for i in range(3):
            lo = 0
            for units in LOADS[i]:
                raw, at = raws[i, lo], 0
                ready = []
                for width, vector, gpsimd in units:
                    ready.append((group(i, raw, at, lo, width, vector, gpsimd), lo, width))
                    at += width
                    lo += width
                for grouped, start, width in ready:
                    quantize(i, grouped, start, width)
                if i == 2 and lo == EARLY_TOKENS:
                    pick(picked_bc, bytes_bc[:, 0:lo], 0, EARLY)
                    pick(picked_words[2], words[2][:, 0:lo], 0, EARLY)
            if i == 0:
                pick(picked_a, bytes_a[:], 0, T)
            if i < 2:
                pick(picked_words[i], words[i][:], 0, T)
        pick(picked_bc, bytes_bc[:], EARLY, FIRST)
        pick(picked_words[2], words[2][:], EARLY, FIRST)
        pick(picked_bc, bytes_bc[:], FIRST, T)
        pick(picked_words[2], words[2][:], FIRST, STARTS[3])
        pick(picked_words[2], words[2][:], STARTS[3], T)

        def multiply(acc, e, m, lo, hi, i, start, stop):
            n_cols = slice(P * m, P * (m + 1))
            if i == 2:
                lhs = w8[:, e, 4 * P * m : 4 * P * (m + 1)].bitcast(FP8X4)
                lhs_scale = s8[:, e, n_cols]
            else:
                lhs = w4[:, e, i, 2 * P * m : 2 * P * (m + 1)].bitcast(FP4X4)
                lhs_scale = s4[:, 2 * e + i, n_cols]
            nc.tensor.matmul_mx(
                out=acc,
                lhsT=lhs,
                lhsT_scale=lhs_scale,
                rhs=picked_words[i][:, lo:hi].bitcast(FP8X4),
                rhs_scale=picked_planes[i][:, lo:hi],
                start=start,
                stop=stop,
            )

        def gelu(dst, acc, e, m):
            nc.scalar.activation(dst, acc, ACT.Gelu_apprx_tanh, bias=bias[:, m, e : e + 1])

        def scatter_product(m, y, lo, hi):
            nc.vector.tensor_tensor(result[m][:].indirect(entries(lo, hi)), y, gates[:, lo:hi], MULT)

        def scatter_copy(m, z, lo, hi):
            nc.scalar.activation(result[m][:].indirect(entries(lo, hi)), z, ACT.Copy)

        result = [keep.tile([P, T], F32, name=f"result{m}") for m in range(2)]

        def first_expert(y, m, lo, hi):
            acc = psum.tile([P, hi - lo], F32, name=f"acc_first{m}")
            for i in range(3):
                multiply(acc[:], 0, m, lo, hi, i, i == 0, i == 2)
            gelu(y, acc[:], 0, m)

        y_early = keep.tile([P, 2, EARLY], F32, name="y_early")
        for m in range(2):
            first_expert(y_early[:, m, :], m, 0, EARLY)
        y_rest = []
        for m in range(2):
            z_early = keep.tile([P, EARLY], F32, name=f"shared{m}")
            nc.gpsimd.tensor_tensor(z_early[:], y_early[:, m, :], gates[:, 0:EARLY], MULT)
            scatter_copy(m, z_early[:], 0, EARLY)
            y_rest.append(keep.tile([P, T - EARLY], F32, name=f"shared{m}"))
            first_expert(y_rest[m][:, 0 : FIRST - EARLY], m, EARLY, FIRST)

        banks = (((1, 1), (1, 0)), ((2, 0),), ((2, 1),), ((3, 1),), ((3, 0),))
        accs = {}
        for n, sums in enumerate(banks):
            bank = psum.tile([P, len(sums), COUNTS[sums[0][0]]], F32, name=f"acc{n}")
            for place, key in enumerate(sums):
                accs[key] = bank[:, place, :]
        for sums in banks:
            for i in (1, 0, 2):
                for e, m in sums:
                    start = i == 1 and (e, m) == sums[0]
                    stop = i == 2 and (e, m) == sums[-1]
                    multiply(accs[e, m], e, m, STARTS[e], STARTS[e + 1], i, start, stop)

        def y_of(m, lo, hi):
            return y_rest[m][:, lo - EARLY : hi - EARLY]

        for sums in banks:
            for e, m in sums:
                gelu(y_of(m, STARTS[e], STARTS[e + 1]), accs[e, m], e, m)

        for m, hi in ((0, FIRST), (1, STARTS[2])):
            scatter_product(m, y_of(m, EARLY, hi), EARLY, hi)
        z = keep.tile([P, STARTS[3] - FIRST], F32, name="z")
        nc.vector.tensor_tensor(z[:], y_of(0, FIRST, STARTS[3]), gates[:, FIRST : STARTS[3]], MULT)
        scatter_copy(0, z[:], FIRST, STARTS[3])
        for m, lo in ((1, STARTS[2]), (0, STARTS[3])):
            scatter_product(m, y_of(m, lo, T), lo, T)
        for m in (1, 0):
            nc.sync.dma_start(out[P * m : P * (m + 1), :], result[m][:])
